import numpy as np
import ml_dtypes


def mxq(x, axis, fmt="e4m3"):
    dtype, down = {"e4m3": (ml_dtypes.float8_e4m3fn, 7), "e5m2": (ml_dtypes.float8_e5m2, 14)}[fmt]
    v = np.moveaxis(np.asarray(x, np.float32).astype(ml_dtypes.bfloat16).astype(np.float64), axis, -1)
    blocks = v.reshape(v.shape[:-1] + (-1, 32))
    amax = np.abs(blocks).max(-1, keepdims=True)
    byte = np.maximum(np.where(amax > 0, np.frexp(amax)[1] - 1 + 127, 0) - down, 1)
    scale = np.exp2(byte - 127.0)
    codes = (blocks / scale).astype(np.float32).astype(dtype).astype(np.float64)
    return np.moveaxis((codes * scale).reshape(v.shape), -1, axis)


WIDE = False


def mx_kscale(k):
    if not WIDE:
        return np.ones(k)
    levels = np.array([18, -18])
    if k % 512:
        return np.exp2(np.random.permutation(np.resize(levels, k // 32))).repeat(32)
    a = np.empty((k // 512, 16))
    for p in range(k // 512):
        a[p, :8] = np.random.permutation(np.resize(levels, 8))
        for g in range(8):
            far = levels[np.abs(levels - a[p, g]) >= 10]
            a[p, g + 8] = far[np.random.randint(len(far))]
    return np.exp2(a.ravel()).repeat(32)


def f64(x):
    return np.asarray(x).astype(np.float64)


def striped(idx):
    return np.tile(np.asarray(idx).reshape(-1, 16).T, (8, 1)).astype(np.uint16)


def unstriped(offs):
    return offs[:16].T.reshape(-1).astype(np.int64)


def setup_inputs():
    n = np.random.standard_normal
    uni = np.random.uniform
    idx = np.random.permutation(1024)[:512]
    f_i = np.ones(1024)
    f_i[idx] = mx_kscale(512)
    f_m = mx_kscale(512)
    return {
        "wo": (n((512, 512)) / np.sqrt(512) * f_m[:, None]).astype(np.float32),
        "dy": (n((512, 512)) / f_m[:, None]).astype(np.float32),
        "dcn": (n((512, 1024))).astype(np.float32),
        "gi": (1.0 / (1.0 + np.exp(-2.5 * n((512, 1024))))).astype(np.float32),
        "gf": (1.0 / (1.0 + np.exp(-2.5 * n((512, 1024))))).astype(np.float32),
        "go": (1.0 / (1.0 + np.exp(-2.5 * n((512, 1024))))).astype(np.float32),
        "gc": (np.tanh(1.5 * n((512, 1024))) * f_i[None, :]).astype(np.float32),
        "ct": (np.tanh(1.5 * n((512, 1024)))).astype(np.float32),
        "cp": (n((512, 1024)) * f_i[None, :]).astype(np.float32),
        "h0": (n((512, 1024)) / f_i[None, :]).astype(np.float32),
        "offs": striped(idx),
    }


def reference(wo, dy, dcn, gi, gf, go, gc, ct, cp, h0, offs):
    idx = unstriped(offs)
    dh = mxq(f64(wo), 0, "e4m3").T @ mxq(f64(dy), 0, "e5m2")
    s_dcn = f64(dcn)[:, idx]
    s_gi = f64(gi)[:, idx]
    s_gf = f64(gf)[:, idx]
    s_go = f64(go)[:, idx]
    s_gc = f64(gc)[:, idx]
    s_ct = f64(ct)[:, idx]
    s_cp = f64(cp)[:, idx]
    dc = s_dcn + dh * s_go * (1.0 - np.square(s_ct))
    zi = dc * s_gc * s_gi * (1.0 - s_gi)
    zf = dc * s_cp * s_gf * (1.0 - s_gf)
    h0_i = f64(h0)[:, idx]
    q_h0_i = mxq(h0_i, 1, "e4m3")
    out_0 = q_h0_i @ mxq(zi, 1, "e5m2").T
    out_1 = q_h0_i @ mxq(zf, 1, "e5m2").T
    return out_0, out_1

@@ -1,0 +1,207 @@
+from contextlib import ExitStack
+
+import concourse.mybir as mybir
+from concourse.masks import make_identity
+
+F32 = mybir.dt.float32
+BF16 = mybir.dt.bfloat16
+U32 = mybir.dt.uint32
+U16 = mybir.dt.uint16
+U8 = mybir.dt.uint8
+E4M3X4 = mybir.dt.float8_e4m3fn_x4
+E5M2X4 = mybir.dt.float8_e5m2_x4
+MULT = mybir.AluOpType.mult
+ADD = mybir.AluOpType.add
+SUB = mybir.AluOpType.subtract
+COPY = mybir.ActivationFunctionType.Copy
+SQUARE = mybir.ActivationFunctionType.Square
+
+P = 128
+PACK = 4
+H = 512
+SLOTS = 512
+SESSIONS = 1024
+TILES = H // P
+FLOPS = 3 * 2 * 512 * 512 * 512
+
+
+def tile_attend_glstm_u_kernel(tc, wo, dy, dcn, gi, gf, go, gc, ct, cp, h0, offs, out_0, out_1):
+    nc = tc.nc
+    with ExitStack() as ctx:
+        keep = ctx.enter_context(tc.tile_pool(name="keep", bufs=1))
+        work = ctx.enter_context(tc.tile_pool(name="work", bufs=2))
+        psum = ctx.enter_context(tc.psum_pool(name="psum", bufs=1))
+
+        offsets = keep.tile([P, SLOTS // 16], U16, name="offsets")
+        ident = keep.tile([P, P], F32, name="ident")
+        make_identity(nc, ident[:])
+
+        def load_rows(table, j):
+            window = work.tile([P, SESSIONS], F32, name="window", tag="window", bufs=24)
+            nc.sync.dma_start(out=window[:], in_=table[j * P : (j + 1) * P, :])
+            return window
+
+        def listed(window):
+            return window[:].indirect(offsets[:])
+
+        def dealt(ap):
+            return ap.rearrange("p (u b x) -> p b u x", u=2, x=16)
+
+        def in_order(ap):
+            return ap.rearrange("p (b u x) -> p b u x", u=2, x=16)
+
+        def turn_and_quantize(dealt_bf16, codes, scales, fmt):
+            words = dealt_bf16[:].bitcast(F32)
+            bank = psum.tile([P, 2, P], F32, name="turn", tag="turn", bufs=2)
+            for u in range(2):
+                nc.tensor.transpose(bank[:, u, :], words[:, u * P : (u + 1) * P], ident[:])
+            grouped = work.tile([P, P * PACK], BF16, name="grouped", tag="grouped", bufs=3, align_bytes=64)
+            nc.scalar.copy(
+                out=grouped[:].bitcast(F32).rearrange("p (c u) -> p c u", u=2),
+                in_=bank[:].rearrange("p u c -> p c u"),
+            )
+            nc.vector.quantize_mx(out=codes.bitcast(fmt), scales=scales, in_=grouped[:])
+
+        def load_first_operand(src):
+            raw = work.tile([P, PACK, 512], F32, name="raw", tag="raw", bufs=2)
+            nc.sync.dma_start(out=raw[:], in_=src.rearrange("(p t) c -> p t c", t=PACK))
+            return raw
+
+        def quantize_first_operand(raw, name, fmt):
+            codes = keep.tile([P, 512], U32, name=name + "_codes", align_bytes=64)
+            scales = keep.tile([P, 512], U8, name=name + "_scales", align_bytes=64)
+            for half in range(2):
+                cols = slice(half * 256, (half + 1) * 256)
+                grouped = work.tile([P, 256 * PACK], BF16, name="grouped_m", tag="grouped_m", bufs=2, align_bytes=64)
+                nc.scalar.copy(
+                    out=grouped[:].rearrange("p (c i t) -> p c t i", i=4, t=PACK),
+                    in_=raw[:, :, cols].rearrange("p t (c i) -> p c t i", i=4),
+                )
+                nc.vector.quantize_mx(out=codes[:, cols].bitcast(fmt), scales=scales[:, cols], in_=grouped[:])
+            return codes, scales
+
+        def gate_factors(j):
+            gates = [load_rows(gi, j), load_rows(gf, j)]
+            partners = [load_rows(gc, j), load_rows(cp, j)]
+            slopes = []
+            for gate in gates:
+                slope = work.tile([P, SLOTS], F32, name="slope", tag="slope", bufs=4)
+                nc.vector.tensor_copy(out=slope[:], in_=listed(gate))
+                slopes.append(slope)
+            for slope in slopes:
+                nc.vector.scalar_tensor_tensor(out=slope[:], in0=slope[:], scalar=1.0, in1=slope[:], op0=SUB, op1=MULT)
+            factors = []
+            for partner, slope in zip(partners, slopes):
+                factor = work.tile([P, SLOTS], F32, name="factor", tag="factor", bufs=2 * TILES)
+                nc.vector.tensor_tensor(out=factor[:], in0=listed(partner), in1=slope[:], op=MULT)
+                factors.append(factor)
+            return factors
+
+        def output_gate_factor(j):
+            ct_rows = load_rows(ct, j)
+            go_rows = load_rows(go, j)
+            tanh_slope = work.tile([P, SLOTS], F32, name="tanh_slope", tag="tanh_slope", bufs=2)
+            nc.vector.tensor_copy(out=tanh_slope[:], in_=listed(ct_rows))
+            nc.scalar.activation(out=tanh_slope[:], in_=tanh_slope[:], func=SQUARE)
+            nc.scalar.activation(out=tanh_slope[:], in_=tanh_slope[:], func=COPY, scale=-1.0, bias=1.0)
+            through = work.tile([P, SLOTS], F32, name="through", tag="through", bufs=TILES)
+            nc.vector.tensor_tensor(out=through[:], in0=listed(go_rows), in1=tanh_slope[:], op=MULT)
+            return through
+
+        def hidden_gradient(j, wo_q, dy_q):
+            cols = slice(j * P, (j + 1) * P)
+            dh = psum.tile([P, SLOTS], F32, name="acc", tag="acc", bufs=6)
+            nc.tensor.matmul_mx(
+                out=dh[:],
+                lhsT=wo_q[0][:, cols].bitcast(E4M3X4),
+                lhsT_scale=wo_q[1][:, cols],
+                rhs=dy_q[0][:].bitcast(E5M2X4),
+                rhs_scale=dy_q[1][:],
+                start=True,
+                stop=True,
+            )
+            return dh
+
+        def gate_gradients(j, dh, through, factors, z_codes, z_scales):
+            dcn_rows = load_rows(dcn, j)
+            nc.vector.tensor_tensor(out=through[:], in0=through[:], in1=dh[:], op=MULT)
+            dc = work.tile([P, SLOTS], F32, name="dc", tag="dc", bufs=2)
+            nc.vector.tensor_tensor(out=dc[:], in0=listed(dcn_rows), in1=through[:], op=ADD)
+            for g, factor in enumerate(factors):
+                z = work.tile([P, SLOTS], BF16, name="z", tag="z", bufs=4, align_bytes=64)
+                nc.vector.tensor_tensor(out=dealt(z[:]), in0=in_order(factor[:]), in1=in_order(dc[:]), op=MULT)
+                block = 2 * g + j % 2
+                cols = slice(block * P, (block + 1) * P)
+                turn_and_quantize(z, z_codes[:, cols], z_scales[:, cols], E5M2X4)
+
+        h0_codes = keep.tile([P, H], U32, name="h0_codes", align_bytes=64)
+        h0_scales = keep.tile([P, H], U8, name="h0_scales", align_bytes=64)
+
+        def old_hidden(k):
+            rows = load_rows(h0, k)
+            rows_bf16 = work.tile([P, SESSIONS], BF16, name="h0_bf16", tag="h0_bf16", bufs=2)
+            nc.scalar.activation(out=rows_bf16[:], in_=rows[:], func=COPY)
+            picked = work.tile([P, SLOTS], BF16, name="h0_picked", tag="h0_picked", bufs=2, align_bytes=64)
+            nc.scalar.activation(out=dealt(picked[:]), in_=listed(rows_bf16), func=COPY)
+            cols = slice(k * P, (k + 1) * P)
+            turn_and_quantize(picked, h0_codes[:, cols], h0_scales[:, cols], E4M3X4)
+
+        def weight_gradients(pair, z_codes, z_scales, last):
+            staged = work.tile([P, PACK, 512], F32, name="raw", tag="raw", bufs=2)
+            h_cols = slice(pair * 256, (pair + 1) * 256)
+            for k in range(TILES):
+                cols = slice(k * P, (k + 1) * P)
+                acc = psum.tile([P, 512], F32, name="acc", tag="acc", bufs=6)
+                nc.tensor.matmul_mx(
+                    out=acc[:],
+                    lhsT=h0_codes[:, cols].bitcast(E4M3X4),
+                    lhsT_scale=h0_scales[:, cols],
+                    rhs=z_codes[:].bitcast(E5M2X4),
+                    rhs_scale=z_scales[:],
+                    start=True,
+                    stop=True,
+                )
+                if last and k % 2 == 1:
+                    nc.vector.tensor_scalar(out=staged[:, k, :], in0=acc[:], scalar1=-1.0, scalar2=None, op0=MULT)
+                else:
+                    nc.scalar.activation(out=staged[:, k, :], in_=acc[:], func=COPY, scale=-1.0)
+                if last:
+                    for g, out in enumerate((out_0, out_1)):
+                        nc.sync.dma_start(out=out[cols, h_cols], in_=staged[:, k, g * 256 : (g + 1) * 256])
+            if not last:
+                for g, out in enumerate((out_0, out_1)):
+                    nc.sync.dma_start(
+                        out=out[:, h_cols].rearrange("(k p) h -> p k h", p=P),
+                        in_=staged[:, :, g * 256 : (g + 1) * 256],
+                    )
+
+        z_q = [
+            (
+                keep.tile([P, 512], U32, name=f"z_codes{pair}", align_bytes=64),
+                keep.tile([P, 512], U8, name=f"z_scales{pair}", align_bytes=64),
+            )
+            for pair in range(2)
+        ]
+
+        nc.sync.dma_start(out=offsets[:], in_=offs)
+        factors = [gate_factors(j) for j in range(3)]
+        dy_raw = load_first_operand(dy)
+        wo_raw = load_first_operand(wo)
+        dy_q = quantize_first_operand(dy_raw, "dy", E5M2X4)
+        wo_q = quantize_first_operand(wo_raw, "wo", E4M3X4)
+        through = [output_gate_factor(0)]
+        factors.append(gate_factors(3))
+        dh = [hidden_gradient(j, wo_q, dy_q) for j in range(TILES)]
+        through.append(output_gate_factor(1))
+        gate_gradients(0, dh[0], through[0], factors[0], *z_q[0])
+        old_hidden(0)
+        old_hidden(1)
+        through.append(output_gate_factor(2))
+        gate_gradients(1, dh[1], through[1], factors[1], *z_q[0])
+        old_hidden(2)
+        old_hidden(3)
+        weight_gradients(0, *z_q[0], last=False)
+        through.append(output_gate_factor(3))
+        gate_gradients(2, dh[2], through[2], factors[2], *z_q[1])
+        gate_gradients(3, dh[3], through[3], factors[3], *z_q[1])
+        weight_gradients(1, *z_q[1], last=True)

@@ -12,7 +12,6 @@ E4M3X4 = mybir.dt.float8_e4m3fn_x4
 E5M2X4 = mybir.dt.float8_e5m2_x4
 MULT = mybir.AluOpType.mult
 ADD = mybir.AluOpType.add
-SUB = mybir.AluOpType.subtract
 COPY = mybir.ActivationFunctionType.Copy
 SQUARE = mybir.ActivationFunctionType.Square
 
@@ -67,12 +66,13 @@ def tile_attend_glstm_u_kernel(tc, wo, dy, dcn, gi, gf, go, gc, ct, cp, h0, offs
             nc.sync.dma_start(out=raw[:], in_=src.rearrange("(p t) c -> p t c", t=PACK))
             return raw
 
-        def quantize_first_operand(raw, name, fmt):
+        def quantize_first_operand(raw, name, fmt, pieces):
             codes = keep.tile([P, 512], U32, name=name + "_codes", align_bytes=64)
             scales = keep.tile([P, 512], U8, name=name + "_scales", align_bytes=64)
-            for half in range(2):
-                cols = slice(half * 256, (half + 1) * 256)
-                grouped = work.tile([P, 256 * PACK], BF16, name="grouped_m", tag="grouped_m", bufs=2, align_bytes=64)
+            width = 512 // pieces
+            for piece in range(pieces):
+                cols = slice(piece * width, (piece + 1) * width)
+                grouped = work.tile([P, width * PACK], BF16, name="grouped_m", tag="grouped_m", bufs=3, align_bytes=64)
                 nc.scalar.copy(
                     out=grouped[:].rearrange("p (c i t) -> p c t i", i=4, t=PACK),
                     in_=raw[:, :, cols].rearrange("p t (c i) -> p c t i", i=4),
@@ -80,33 +80,33 @@ def tile_attend_glstm_u_kernel(tc, wo, dy, dcn, gi, gf, go, gc, ct, cp, h0, offs
                 nc.vector.quantize_mx(out=codes[:, cols].bitcast(fmt), scales=scales[:, cols], in_=grouped[:])
             return codes, scales
 
-        def gate_factors(j):
-            gates = [load_rows(gi, j), load_rows(gf, j)]
-            partners = [load_rows(gc, j), load_rows(cp, j)]
-            slopes = []
-            for gate in gates:
-                slope = work.tile([P, SLOTS], F32, name="slope", tag="slope", bufs=4)
-                nc.vector.tensor_copy(out=slope[:], in_=listed(gate))
-                slopes.append(slope)
-            for slope in slopes:
-                nc.vector.scalar_tensor_tensor(out=slope[:], in0=slope[:], scalar=1.0, in1=slope[:], op0=SUB, op1=MULT)
-            factors = []
-            for partner, slope in zip(partners, slopes):
-                factor = work.tile([P, SLOTS], F32, name="factor", tag="factor", bufs=2 * TILES)
-                nc.vector.tensor_tensor(out=factor[:], in0=listed(partner), in1=slope[:], op=MULT)
-                factors.append(factor)
-            return factors
+        def gate_slope(table, j):
+            rows = load_rows(table, j)
+            gate = work.tile([P, SLOTS], F32, name="gate", tag="gate", bufs=3)
+            nc.vector.tensor_copy(out=gate[:], in_=listed(rows))
+            slope = work.tile([P, SLOTS], F32, name="slope", tag="slope", bufs=6)
+            nc.scalar.activation(out=slope[:], in_=gate[:], func=COPY, scale=-1.0, bias=1.0)
+            nc.gpsimd.tensor_tensor(out=slope[:], in0=gate[:], in1=slope[:], op=MULT)
+            return slope[:]
 
-        def output_gate_factor(j):
-            ct_rows = load_rows(ct, j)
-            go_rows = load_rows(go, j)
-            tanh_slope = work.tile([P, SLOTS], F32, name="tanh_slope", tag="tanh_slope", bufs=2)
-            nc.vector.tensor_copy(out=tanh_slope[:], in_=listed(ct_rows))
-            nc.scalar.activation(out=tanh_slope[:], in_=tanh_slope[:], func=SQUARE)
-            nc.scalar.activation(out=tanh_slope[:], in_=tanh_slope[:], func=COPY, scale=-1.0, bias=1.0)
-            through = work.tile([P, SLOTS], F32, name="through", tag="through", bufs=TILES)
-            nc.vector.tensor_tensor(out=through[:], in0=listed(go_rows), in1=tanh_slope[:], op=MULT)
-            return through
+        def tanh_slope(j):
+            rows = load_rows(ct, j)
+            slope = work.tile([P, SLOTS], F32, name="slope", tag="slope", bufs=6)
+            nc.vector.tensor_copy(out=slope[:], in_=listed(rows))
+            nc.scalar.activation(out=slope[:], in_=slope[:], func=SQUARE)
+            nc.scalar.activation(out=slope[:], in_=slope[:], func=COPY, scale=-1.0, bias=1.0)
+            return slope[:]
+
+        def slopes_of(pair):
+            tiles = (2 * pair, 2 * pair + 1)
+            gates = [[gate_slope(table, j) for table in (gi, gf)] for j in tiles]
+            return [gates[n] + [tanh_slope(j)] for n, j in enumerate(tiles)]
+
+        def listed_times(table, j, slope):
+            rows = load_rows(table, j)
+            factor = work.tile([P, SLOTS], F32, name="factor", tag="factor", bufs=3 * TILES)
+            nc.vector.tensor_tensor(out=factor[:], in0=listed(rows), in1=slope, op=MULT)
+            return factor
 
         def hidden_gradient(j, wo_q, dy_q):
             cols = slice(j * P, (j + 1) * P)
@@ -122,9 +122,8 @@ def tile_attend_glstm_u_kernel(tc, wo, dy, dcn, gi, gf, go, gc, ct, cp, h0, offs
             )
             return dh
 
-        def gate_gradients(j, dh, through, factors, z_codes, z_scales):
+        def gate_gradients(j, through, factors, z_codes, z_scales):
             dcn_rows = load_rows(dcn, j)
-            nc.vector.tensor_tensor(out=through[:], in0=through[:], in1=dh[:], op=MULT)
             dc = work.tile([P, SLOTS], F32, name="dc", tag="dc", bufs=2)
             nc.vector.tensor_tensor(out=dc[:], in0=listed(dcn_rows), in1=through[:], op=ADD)
             for g, factor in enumerate(factors):
@@ -162,9 +161,9 @@ def tile_attend_glstm_u_kernel(tc, wo, dy, dcn, gi, gf, go, gc, ct, cp, h0, offs
                     stop=True,
                 )
                 if last and k % 2 == 1:
-                    nc.vector.tensor_scalar(out=staged[:, k, :], in0=acc[:], scalar1=-1.0, scalar2=None, op0=MULT)
+                    nc.vector.tensor_copy(out=staged[:, k, :], in_=acc[:])
                 else:
-                    nc.scalar.activation(out=staged[:, k, :], in_=acc[:], func=COPY, scale=-1.0)
+                    nc.scalar.copy(out=staged[:, k, :], in_=acc[:])
                 if last:
                     for g, out in enumerate((out_0, out_1)):
                         nc.sync.dma_start(out=out[cols, h_cols], in_=staged[:, k, g * 256 : (g + 1) * 256])
@@ -184,24 +183,29 @@ def tile_attend_glstm_u_kernel(tc, wo, dy, dcn, gi, gf, go, gc, ct, cp, h0, offs
         ]
 
         nc.sync.dma_start(out=offsets[:], in_=offs)
-        factors = [gate_factors(j) for j in range(3)]
-        dy_raw = load_first_operand(dy)
-        wo_raw = load_first_operand(wo)
-        dy_q = quantize_first_operand(dy_raw, "dy", E5M2X4)
-        wo_q = quantize_first_operand(wo_raw, "wo", E4M3X4)
-        through = [output_gate_factor(0)]
-        factors.append(gate_factors(3))
-        dh = [hidden_gradient(j, wo_q, dy_q) for j in range(TILES)]
-        through.append(output_gate_factor(1))
-        gate_gradients(0, dh[0], through[0], factors[0], *z_q[0])
+        def times_dh(through, dh):
+            nc.vector.tensor_tensor(out=through[:], in0=through[:], in1=dh[:], op=MULT)
+
+        slopes = slopes_of(0)
+        factors = [[listed_times(table, j, slope) for table, slope in zip((gc, cp, go), slopes[j])] for j in range(2)]
         old_hidden(0)
+        slopes = slopes_of(1)
+        dy_q = quantize_first_operand(load_first_operand(dy), "dy", E5M2X4, 2)
+        factors.append([listed_times(gc, 2, slopes[0][0]), listed_times(cp, 2, slopes[0][1])])
+        wo_q = quantize_first_operand(load_first_operand(wo), "wo", E4M3X4, 4)
+        dh = [hidden_gradient(j, wo_q, dy_q) for j in range(TILES)]
+        factors[2].append(listed_times(go, 2, slopes[0][2]))
+        last_i = listed_times(gc, 3, slopes[1][0])
+        for j in range(3):
+            times_dh(factors[j][2], dh[j])
         old_hidden(1)
-        through.append(output_gate_factor(2))
-        gate_gradients(1, dh[1], through[1], factors[1], *z_q[0])
+        last_f = listed_times(cp, 3, slopes[1][1])
         old_hidden(2)
-        old_hidden(3)
-        weight_gradients(0, *z_q[0], last=False)
-        through.append(output_gate_factor(3))
-        gate_gradients(2, dh[2], through[2], factors[2], *z_q[1])
-        gate_gradients(3, dh[3], through[3], factors[3], *z_q[1])
-        weight_gradients(1, *z_q[1], last=True)
+        factors.append([last_i, last_f, listed_times(go, 3, slopes[1][2])])
+        times_dh(factors[3][2], dh[3])
+        for j in range(TILES):
+            gate_gradients(j, factors[j][2], factors[j][:2], *z_q[j // 2])
+            if j == 0:
+                old_hidden(3)
+            if j % 2 == 1:
+                weight_gradients(j // 2, *z_q[j // 2], last=(j == 3))

@@ -17,11 +17,10 @@ SQUARE = mybir.ActivationFunctionType.Square
 
 P = 128
 PACK = 4
-H = 512
-SLOTS = 512
+WIDTH = 512
 SESSIONS = 1024
-TILES = H // P
-FLOPS = 3 * 2 * 512 * 512 * 512
+TILES = WIDTH // P
+FLOPS = 3 * 2 * WIDTH * WIDTH * WIDTH
 
 
 def tile_attend_glstm_u_kernel(tc, wo, dy, dcn, gi, gf, go, gc, ct, cp, h0, offs, out_0, out_1):
@@ -31,13 +30,30 @@ def tile_attend_glstm_u_kernel(tc, wo, dy, dcn, gi, gf, go, gc, ct, cp, h0, offs
         work = ctx.enter_context(tc.tile_pool(name="work", bufs=2))
         psum = ctx.enter_context(tc.psum_pool(name="psum", bufs=1))
 
-        offsets = keep.tile([P, SLOTS // 16], U16, name="offsets")
+        offsets = keep.tile([P, WIDTH // 16], U16, name="offsets")
         ident = keep.tile([P, P], F32, name="ident")
         make_identity(nc, ident[:])
 
+        def quantized(name, columns):
+            codes = keep.tile([P, columns], U32, name=name + "_codes", align_bytes=64)
+            scales = keep.tile([P, columns], U8, name=name + "_scales", align_bytes=64)
+            return codes, scales
+
+        wo_q = quantized("wo", WIDTH)
+        dy_q = quantized("dy", WIDTH)
+        h0_q = quantized("h0", WIDTH)
+        z_q = quantized("z", 2 * WIDTH)
+        h0_grouped = keep.tile([P, WIDTH * PACK], BF16, name="h0_grouped", align_bytes=64)
+        z_grouped = keep.tile([P, 2 * WIDTH * PACK], BF16, name="z_grouped", align_bytes=64)
+        turn_bank = psum.tile([P, 4, P], F32, name="turn_bank")
+        last_bank = psum.tile([P, 2, P], F32, name="last_bank")
+
+        def blocks(first, count=1):
+            return slice(first * P, (first + count) * P)
+
         def load_rows(table, j):
-            window = work.tile([P, SESSIONS], F32, name="window", tag="window", bufs=24)
-            nc.sync.dma_start(out=window[:], in_=table[j * P : (j + 1) * P, :])
+            window = work.tile([P, SESSIONS], F32, name="window", bufs=24)
+            nc.sync.dma_start(out=window[:], in_=table[blocks(j), :])
             return window
 
         def listed(window):
@@ -49,163 +65,165 @@ def tile_attend_glstm_u_kernel(tc, wo, dy, dcn, gi, gf, go, gc, ct, cp, h0, offs
         def in_order(ap):
             return ap.rearrange("p (b u x) -> p b u x", u=2, x=16)
 
-        def turn_and_quantize(dealt_bf16, codes, scales, fmt):
-            words = dealt_bf16[:].bitcast(F32)
-            bank = psum.tile([P, 2, P], F32, name="turn", tag="turn", bufs=2)
-            for u in range(2):
-                nc.tensor.transpose(bank[:, u, :], words[:, u * P : (u + 1) * P], ident[:])
-            grouped = work.tile([P, P * PACK], BF16, name="grouped", tag="grouped", bufs=3, align_bytes=64)
-            nc.scalar.copy(
-                out=grouped[:].bitcast(F32).rearrange("p (c u) -> p c u", u=2),
-                in_=bank[:].rearrange("p u c -> p c u"),
-            )
-            nc.vector.quantize_mx(out=codes.bitcast(fmt), scales=scales, in_=grouped[:])
+        def quantize(operand, cols, grouped, fmt):
+            codes, scales = operand
+            nc.vector.quantize_mx(out=codes[:, cols].bitcast(fmt), scales=scales[:, cols], in_=grouped)
 
-        def load_first_operand(src):
-            raw = work.tile([P, PACK, 512], F32, name="raw", tag="raw", bufs=2)
-            nc.sync.dma_start(out=raw[:], in_=src.rearrange("(p t) c -> p t c", t=PACK))
-            return raw
-
-        def quantize_first_operand(raw, name, fmt, pieces):
-            codes = keep.tile([P, 512], U32, name=name + "_codes", align_bytes=64)
-            scales = keep.tile([P, 512], U8, name=name + "_scales", align_bytes=64)
-            width = 512 // pieces
-            for piece in range(pieces):
-                cols = slice(piece * width, (piece + 1) * width)
-                grouped = work.tile([P, width * PACK], BF16, name="grouped_m", tag="grouped_m", bufs=3, align_bytes=64)
-                nc.scalar.copy(
-                    out=grouped[:].rearrange("p (c i t) -> p c t i", i=4, t=PACK),
-                    in_=raw[:, :, cols].rearrange("p t (c i) -> p c t i", i=4),
-                )
-                nc.vector.quantize_mx(out=codes[:, cols].bitcast(fmt), scales=scales[:, cols], in_=grouped[:])
-            return codes, scales
-
-        def gate_slope(table, j):
-            rows = load_rows(table, j)
-            gate = work.tile([P, SLOTS], F32, name="gate", tag="gate", bufs=3)
-            nc.vector.tensor_copy(out=gate[:], in_=listed(rows))
-            slope = work.tile([P, SLOTS], F32, name="slope", tag="slope", bufs=6)
-            nc.scalar.activation(out=slope[:], in_=gate[:], func=COPY, scale=-1.0, bias=1.0)
-            nc.gpsimd.tensor_tensor(out=slope[:], in0=gate[:], in1=slope[:], op=MULT)
-            return slope[:]
-
-        def tanh_slope(j):
-            rows = load_rows(ct, j)
-            slope = work.tile([P, SLOTS], F32, name="slope", tag="slope", bufs=6)
-            nc.vector.tensor_copy(out=slope[:], in_=listed(rows))
-            nc.scalar.activation(out=slope[:], in_=slope[:], func=SQUARE)
-            nc.scalar.activation(out=slope[:], in_=slope[:], func=COPY, scale=-1.0, bias=1.0)
-            return slope[:]
-
-        def slopes_of(pair):
-            tiles = (2 * pair, 2 * pair + 1)
-            gates = [[gate_slope(table, j) for table in (gi, gf)] for j in tiles]
-            return [gates[n] + [tanh_slope(j)] for n, j in enumerate(tiles)]
-
-        def listed_times(table, j, slope):
-            rows = load_rows(table, j)
-            factor = work.tile([P, SLOTS], F32, name="factor", tag="factor", bufs=3 * TILES)
-            nc.vector.tensor_tensor(out=factor[:], in0=listed(rows), in1=slope, op=MULT)
-            return factor
-
-        def hidden_gradient(j, wo_q, dy_q):
-            cols = slice(j * P, (j + 1) * P)
-            dh = psum.tile([P, SLOTS], F32, name="acc", tag="acc", bufs=6)
+        def product(lhs, lhs_cols, lhs_fmt, rhs, rhs_cols, rhs_fmt):
+            acc = psum.tile([P, WIDTH], F32, name="acc", bufs=6)
             nc.tensor.matmul_mx(
-                out=dh[:],
-                lhsT=wo_q[0][:, cols].bitcast(E4M3X4),
-                lhsT_scale=wo_q[1][:, cols],
-                rhs=dy_q[0][:].bitcast(E5M2X4),
-                rhs_scale=dy_q[1][:],
+                out=acc[:],
+                lhsT=lhs[0][:, lhs_cols].bitcast(lhs_fmt),
+                lhsT_scale=lhs[1][:, lhs_cols],
+                rhs=rhs[0][:, rhs_cols].bitcast(rhs_fmt),
+                rhs_scale=rhs[1][:, rhs_cols],
                 start=True,
                 stop=True,
             )
-            return dh
+            return acc
 
-        def gate_gradients(j, through, factors, z_codes, z_scales):
-            dcn_rows = load_rows(dcn, j)
-            dc = work.tile([P, SLOTS], F32, name="dc", tag="dc", bufs=2)
-            nc.vector.tensor_tensor(out=dc[:], in0=listed(dcn_rows), in1=through[:], op=ADD)
-            for g, factor in enumerate(factors):
-                z = work.tile([P, SLOTS], BF16, name="z", tag="z", bufs=4, align_bytes=64)
-                nc.vector.tensor_tensor(out=dealt(z[:]), in0=in_order(factor[:]), in1=in_order(dc[:]), op=MULT)
-                block = 2 * g + j % 2
-                cols = slice(block * P, (block + 1) * P)
-                turn_and_quantize(z, z_codes[:, cols], z_scales[:, cols], E5M2X4)
+        def quantize_along_m(src, operand, cols, fmt, tag):
+            columns = cols.stop - cols.start
+            raw = work.tile([P, PACK, columns], F32, name="raw", tag=tag)
+            nc.sync.dma_start(out=raw[:], in_=src[:, cols].rearrange("(p t) c -> p t c", t=PACK))
+            grouped = work.tile([P, columns * PACK], BF16, name="grouped_m", bufs=3, align_bytes=64)
+            nc.scalar.copy(
+                out=grouped[:].rearrange("p (c i t) -> p c t i", i=4, t=PACK),
+                in_=raw[:].rearrange("p t (c i) -> p c t i", i=4),
+            )
+            quantize(operand, cols, grouped[:], fmt)
 
-        h0_codes = keep.tile([P, H], U32, name="h0_codes", align_bytes=64)
-        h0_scales = keep.tile([P, H], U8, name="h0_scales", align_bytes=64)
+        def turn(dealt_bf16, grouped, bank, copy):
+            words = dealt_bf16[:].bitcast(F32)
+            count = dealt_bf16.shape[1] // WIDTH
+            for n in range(2 * count):
+                nc.tensor.transpose(bank[:, n, :], words[:, blocks(n)], ident[:])
+            copy(
+                out=grouped.bitcast(F32).rearrange("p (g c u) -> p g c u", g=count, u=2),
+                in_=bank[:, : 2 * count, :].rearrange("p (g u) c -> p g c u", u=2),
+            )
+
+        def gate_slope(rows):
+            gate = work.tile([P, WIDTH], F32, name="gate", bufs=3)
+            nc.vector.tensor_copy(out=gate[:], in_=listed(rows))
+            slope = work.tile([P, WIDTH], F32, name="slope", bufs=3 * TILES)
+            nc.scalar.activation(out=slope[:], in_=gate[:], func=COPY, scale=-1.0, bias=1.0)
+            nc.gpsimd.tensor_tensor(out=slope[:], in0=gate[:], in1=slope[:], op=MULT)
+            return slope
+
+        def tanh_slope(rows):
+            slope = work.tile([P, WIDTH], F32, name="slope", bufs=3 * TILES)
+            nc.vector.tensor_copy(out=slope[:], in_=listed(rows))
+            nc.scalar.activation(out=slope[:], in_=slope[:], func=SQUARE)
+            nc.scalar.activation(out=slope[:], in_=slope[:], func=COPY, scale=-1.0, bias=1.0)
+            return slope
+
+        partner = {"i": gc, "f": cp, "o": go}
+        slopes = {}
+        factors = {}
+
+        def make_factor(gate, j):
+            rows = load_rows(partner[gate], j)
+            factor = work.tile([P, WIDTH], F32, name="factor", bufs=3 * TILES)
+            nc.vector.tensor_tensor(out=factor[:], in0=listed(rows), in1=slopes[gate, j][:], op=MULT)
+            factors[gate, j] = factor
+
+        def times_dh(j):
+            dh = product(wo_q, blocks(j), E4M3X4, dy_q, blocks(0, TILES), E5M2X4)
+            through = factors["o", j]
+            nc.vector.tensor_tensor(out=through[:], in0=through[:], in1=dh[:], op=MULT)
+
+        def cell_gradient(j):
+            rows = load_rows(dcn, j)
+            dc = work.tile([P, WIDTH], F32, name="dc")
+            nc.vector.tensor_tensor(out=dc[:], in0=listed(rows), in1=factors["o", j][:], op=ADD)
+            return dc
+
+        def gate_gradients(dc, j, gates):
+            z = work.tile([P, len(gates) * WIDTH], BF16, name="z", bufs=4, align_bytes=64)
+            for n, gate in enumerate(gates):
+                nc.vector.tensor_tensor(
+                    out=dealt(z[:, n * WIDTH : (n + 1) * WIDTH]),
+                    in0=in_order(factors[gate, j][:]),
+                    in1=in_order(dc[:]),
+                    op=MULT,
+                )
+            return z
+
+        def grouped_blocks(grouped, first, count):
+            return grouped[:, first * WIDTH : (first + count) * WIDTH]
+
+        def turn_z(z, first, bank, copy):
+            turn(z, grouped_blocks(z_grouped, first, z.shape[1] // WIDTH), bank, copy)
+
+        def quantize_z(first, count):
+            quantize(z_q, blocks(first, count), grouped_blocks(z_grouped, first, count), E5M2X4)
 
         def old_hidden(k):
             rows = load_rows(h0, k)
-            rows_bf16 = work.tile([P, SESSIONS], BF16, name="h0_bf16", tag="h0_bf16", bufs=2)
+            rows_bf16 = work.tile([P, SESSIONS], BF16, name="h0_bf16")
             nc.scalar.activation(out=rows_bf16[:], in_=rows[:], func=COPY)
-            picked = work.tile([P, SLOTS], BF16, name="h0_picked", tag="h0_picked", bufs=2, align_bytes=64)
+            picked = work.tile([P, WIDTH], BF16, name="h0_picked", align_bytes=64)
             nc.scalar.activation(out=dealt(picked[:]), in_=listed(rows_bf16), func=COPY)
-            cols = slice(k * P, (k + 1) * P)
-            turn_and_quantize(picked, h0_codes[:, cols], h0_scales[:, cols], E4M3X4)
+            turn(picked, grouped_blocks(h0_grouped, k, 1), turn_bank, nc.scalar.copy)
 
-        def weight_gradients(pair, z_codes, z_scales, last):
-            staged = work.tile([P, PACK, 512], F32, name="raw", tag="raw", bufs=2)
-            h_cols = slice(pair * 256, (pair + 1) * 256)
+        def outputs(pair, copies, step):
+            staged = work.tile([P, TILES, WIDTH], F32, name="staged", tag="raw")
             for k in range(TILES):
-                cols = slice(k * P, (k + 1) * P)
-                acc = psum.tile([P, 512], F32, name="acc", tag="acc", bufs=6)
-                nc.tensor.matmul_mx(
-                    out=acc[:],
-                    lhsT=h0_codes[:, cols].bitcast(E4M3X4),
-                    lhsT_scale=h0_scales[:, cols],
-                    rhs=z_codes[:].bitcast(E5M2X4),
-                    rhs_scale=z_scales[:],
-                    start=True,
-                    stop=True,
+                acc = product(h0_q, blocks(k), E4M3X4, z_q, blocks(4 * pair, 4), E5M2X4)
+                copies[k % len(copies)](
+                    out=staged[:, k, :].rearrange("p (g j c) -> p g j c", g=2, j=2),
+                    in_=acc[:].rearrange("p (j g c) -> p g j c", g=2, j=2),
                 )
-                if last and k % 2 == 1:
-                    nc.vector.tensor_copy(out=staged[:, k, :], in_=acc[:])
-                else:
-                    nc.scalar.copy(out=staged[:, k, :], in_=acc[:])
-                if last:
+                if k % step == step - 1:
+                    first = k + 1 - step
                     for g, out in enumerate((out_0, out_1)):
-                        nc.sync.dma_start(out=out[cols, h_cols], in_=staged[:, k, g * 256 : (g + 1) * 256])
-            if not last:
-                for g, out in enumerate((out_0, out_1)):
-                    nc.sync.dma_start(
-                        out=out[:, h_cols].rearrange("(k p) h -> p k h", p=P),
-                        in_=staged[:, :, g * 256 : (g + 1) * 256],
-                    )
+                        nc.sync.dma_start(
+                            out=out[blocks(first, step), blocks(2 * pair, 2)].rearrange("(k p) h -> p k h", p=P),
+                            in_=staged[:, first : k + 1, blocks(2 * g, 2)],
+                        )
 
-        z_q = [
-            (
-                keep.tile([P, 512], U32, name=f"z_codes{pair}", align_bytes=64),
-                keep.tile([P, 512], U8, name=f"z_scales{pair}", align_bytes=64),
-            )
-            for pair in range(2)
-        ]
-
+        first_rows = load_rows(gi, 0)
         nc.sync.dma_start(out=offsets[:], in_=offs)
-        def times_dh(through, dh):
-            nc.vector.tensor_tensor(out=through[:], in0=through[:], in1=dh[:], op=MULT)
-
-        slopes = slopes_of(0)
-        factors = [[listed_times(table, j, slope) for table, slope in zip((gc, cp, go), slopes[j])] for j in range(2)]
-        old_hidden(0)
-        slopes = slopes_of(1)
-        dy_q = quantize_first_operand(load_first_operand(dy), "dy", E5M2X4, 2)
-        factors.append([listed_times(gc, 2, slopes[0][0]), listed_times(cp, 2, slopes[0][1])])
-        wo_q = quantize_first_operand(load_first_operand(wo), "wo", E4M3X4, 4)
-        dh = [hidden_gradient(j, wo_q, dy_q) for j in range(TILES)]
-        factors[2].append(listed_times(go, 2, slopes[0][2]))
-        last_i = listed_times(gc, 3, slopes[1][0])
-        for j in range(3):
-            times_dh(factors[j][2], dh[j])
-        old_hidden(1)
-        last_f = listed_times(cp, 3, slopes[1][1])
-        old_hidden(2)
-        factors.append([last_i, last_f, listed_times(go, 3, slopes[1][2])])
-        times_dh(factors[3][2], dh[3])
         for j in range(TILES):
-            gate_gradients(j, factors[j][2], factors[j][:2], *z_q[j // 2])
-            if j == 0:
-                old_hidden(3)
-            if j % 2 == 1:
-                weight_gradients(j // 2, *z_q[j // 2], last=(j == 3))
+            slopes["i", j] = gate_slope(first_rows if j == 0 else load_rows(gi, j))
+            slopes["f", j] = gate_slope(load_rows(gf, j))
+        for j in range(TILES):
+            slopes["o", j] = tanh_slope(load_rows(ct, j))
+        for gate in "ifo":
+            make_factor(gate, 0)
+        quantize_along_m(dy, dy_q, blocks(0, TILES), E5M2X4, "raw")
+        make_factor("i", 1)
+        quantize_along_m(wo, wo_q, blocks(0, 2), E4M3X4, "wo_raw")
+        make_factor("f", 1)
+        make_factor("o", 1)
+        times_dh(0)
+        times_dh(1)
+        old_hidden(0)
+        z0 = gate_gradients(cell_gradient(0), 0, "if")
+        old_hidden(1)
+        turn_z(z0, 0, turn_bank, nc.scalar.copy)
+        z1 = gate_gradients(cell_gradient(1), 1, "if")
+        old_hidden(2)
+        make_factor("o", 2)
+        quantize_along_m(wo, wo_q, blocks(2, 2), E4M3X4, "wo_raw")
+        make_factor("o", 3)
+        make_factor("i", 2)
+        times_dh(2)
+        times_dh(3)
+        old_hidden(3)
+        quantize(h0_q, blocks(0, TILES), h0_grouped[:], E4M3X4)
+        turn_z(z1, 2, turn_bank, nc.scalar.copy)
+        quantize_z(0, 4)
+        make_factor("f", 2)
+        turn_z(gate_gradients(cell_gradient(2), 2, "if"), 4, turn_bank, nc.scalar.copy)
+        quantize_z(4, 2)
+        outputs(0, [nc.scalar.copy], 2)
+        make_factor("i", 3)
+        make_factor("f", 3)
+        dc = cell_gradient(3)
+        turn_z(gate_gradients(dc, 3, "i"), 6, turn_bank, nc.scalar.copy)
+        quantize_z(6, 1)
+        turn_z(gate_gradients(dc, 3, "f"), 7, last_bank, nc.vector.tensor_copy)
+        quantize_z(7, 1)
+        outputs(1, [nc.scalar.copy, nc.vector.tensor_copy], 1)

@@ -167,21 +167,42 @@ def tile_attend_glstm_u_kernel(tc, wo, dy, dcn, gi, gf, go, gc, ct, cp, h0, offs
             nc.scalar.activation(out=dealt(picked[:]), in_=listed(rows_bf16), func=COPY)
             turn(picked, grouped_blocks(h0_grouped, k, 1), turn_bank, nc.scalar.copy)
 
-        def outputs(pair, copies, step):
-            staged = work.tile([P, TILES, WIDTH], F32, name="staged", tag="raw")
+        def store(out, first, count, cols, staged):
+            nc.sync.dma_start(out=out[blocks(first, count), cols].rearrange("(k p) h -> p k h", p=P), in_=staged)
+
+        def outputs_of_tile_0():
+            for g, out in enumerate((out_0, out_1)):
+                acc = product(z_q, blocks(g), E5M2X4, h0_q, blocks(0, TILES), E4M3X4)
+                by_h = work.tile([P, WIDTH], F32, name="by_h")
+                nc.scalar.copy(out=by_h[:], in_=acc[:])
+                back = psum.tile([P, TILES, P], F32, name="acc", bufs=6)
+                for k in range(TILES):
+                    nc.tensor.transpose(back[:, k, :], by_h[:, blocks(k)], ident[:])
+                staged = work.tile([P, TILES, P], F32, name="staged_0")
+                nc.scalar.copy(out=staged[:], in_=back[:])
+                store(out, 0, TILES, blocks(0), staged[:])
+
+        def outputs_of_tiles_1_2():
+            staged = work.tile([P, TILES, WIDTH], F32, name="staged_1_2", tag="raw")
             for k in range(TILES):
-                acc = product(h0_q, blocks(k), E4M3X4, z_q, blocks(4 * pair, 4), E5M2X4)
-                copies[k % len(copies)](
+                acc = product(h0_q, blocks(k), E4M3X4, z_q, blocks(2, 4), E5M2X4)
+                nc.scalar.copy(
                     out=staged[:, k, :].rearrange("p (g j c) -> p g j c", g=2, j=2),
                     in_=acc[:].rearrange("p (j g c) -> p g j c", g=2, j=2),
                 )
-                if k % step == step - 1:
-                    first = k + 1 - step
+                if k % 2 == 1:
                     for g, out in enumerate((out_0, out_1)):
-                        nc.sync.dma_start(
-                            out=out[blocks(first, step), blocks(2 * pair, 2)].rearrange("(k p) h -> p k h", p=P),
-                            in_=staged[:, first : k + 1, blocks(2 * g, 2)],
-                        )
+                        store(out, k - 1, 2, blocks(1, 2), staged[:, k - 1 : k + 1, blocks(2 * g, 2)])
+
+        def outputs_of_tile_3():
+            staged = work.tile([P, TILES, 2 * P], F32, name="staged_3", tag="raw")
+            for k in range(TILES):
+                acc = product(h0_q, blocks(k), E4M3X4, z_q, blocks(4, 4), E5M2X4)
+                copy = nc.vector.tensor_copy if k % 2 else nc.scalar.copy
+                copy(out=staged[:, k, :], in_=acc[:, blocks(2, 2)])
+                if k % 2 == 1:
+                    for g, out in enumerate((out_0, out_1)):
+                        store(out, k - 1, 2, blocks(3), staged[:, k - 1 : k + 1, blocks(g)])
 
         first_rows = load_rows(gi, 0)
         nc.sync.dma_start(out=offsets[:], in_=offs)
@@ -213,17 +234,18 @@ def tile_attend_glstm_u_kernel(tc, wo, dy, dcn, gi, gf, go, gc, ct, cp, h0, offs
         times_dh(3)
         old_hidden(3)
         quantize(h0_q, blocks(0, TILES), h0_grouped[:], E4M3X4)
+        quantize_z(0, 2)
         turn_z(z1, 2, turn_bank, nc.scalar.copy)
-        quantize_z(0, 4)
         make_factor("f", 2)
         turn_z(gate_gradients(cell_gradient(2), 2, "if"), 4, turn_bank, nc.scalar.copy)
-        quantize_z(4, 2)
-        outputs(0, [nc.scalar.copy], 2)
+        quantize_z(2, 4)
+        outputs_of_tile_0()
+        outputs_of_tiles_1_2()
         make_factor("i", 3)
         make_factor("f", 3)
         dc = cell_gradient(3)
-        turn_z(gate_gradients(dc, 3, "i"), 6, turn_bank, nc.scalar.copy)
+        turn_z(gate_gradients(dc, 3, "i"), 6, turn_bank, nc.vector.tensor_copy)
         quantize_z(6, 1)
         turn_z(gate_gradients(dc, 3, "f"), 7, last_bank, nc.vector.tensor_copy)
         quantize_z(7, 1)
-        outputs(1, [nc.scalar.copy, nc.vector.tensor_copy], 1)
+        outputs_of_tile_3()

@@ -20,6 +20,10 @@ PACK = 4
 WIDTH = 512
 SESSIONS = 1024
 TILES = WIDTH // P
+RUN = 16
+NEIGHBOURS = 4
+WINDOWS = 24
+ACC_BANKS = 6
 FLOPS = 3 * 2 * WIDTH * WIDTH * WIDTH
 
 
@@ -48,29 +52,30 @@ def tile_attend_glstm_u_kernel(tc, wo, dy, dcn, gi, gf, go, gc, ct, cp, h0, offs
         turn_bank = psum.tile([P, 4, P], F32, name="turn_bank")
         last_bank = psum.tile([P, 2, P], F32, name="last_bank")
 
-        def blocks(first, count=1):
+        def strips(first, count=1):
             return slice(first * P, (first + count) * P)
 
         def load_rows(table, j):
-            window = work.tile([P, SESSIONS], F32, name="window", bufs=24)
-            nc.sync.dma_start(out=window[:], in_=table[blocks(j), :])
+            window = work.tile([P, SESSIONS], F32, name="window", bufs=WINDOWS)
+            nc.sync.dma_start(out=window[:], in_=table[strips(j), :])
             return window
 
         def listed(window):
             return window[:].indirect(offsets[:])
 
-        def dealt(ap):
-            return ap.rearrange("p (u b x) -> p b u x", u=2, x=16)
-
         def in_order(ap):
-            return ap.rearrange("p (b u x) -> p b u x", u=2, x=16)
+            return ap.rearrange("p (b u x) -> p b u x", u=2, x=RUN)
+
+        def dealt(ap):
+            return ap.rearrange("p (u b x) -> p b u x", u=2, x=RUN)
 
         def quantize(operand, cols, grouped, fmt):
             codes, scales = operand
             nc.vector.quantize_mx(out=codes[:, cols].bitcast(fmt), scales=scales[:, cols], in_=grouped)
 
-        def product(lhs, lhs_cols, lhs_fmt, rhs, rhs_cols, rhs_fmt):
-            acc = psum.tile([P, WIDTH], F32, name="acc", bufs=6)
+        def product(lhs, lhs_cols, lhs_fmt, rhs, rhs_cols, rhs_fmt, acc=None):
+            if acc is None:
+                acc = psum.tile([P, WIDTH], F32, name="acc", bufs=ACC_BANKS)
             nc.tensor.matmul_mx(
                 out=acc[:],
                 lhsT=lhs[0][:, lhs_cols].bitcast(lhs_fmt),
@@ -88,8 +93,8 @@ def tile_attend_glstm_u_kernel(tc, wo, dy, dcn, gi, gf, go, gc, ct, cp, h0, offs
             nc.sync.dma_start(out=raw[:], in_=src[:, cols].rearrange("(p t) c -> p t c", t=PACK))
             grouped = work.tile([P, columns * PACK], BF16, name="grouped_m", bufs=3, align_bytes=64)
             nc.scalar.copy(
-                out=grouped[:].rearrange("p (c i t) -> p c t i", i=4, t=PACK),
-                in_=raw[:].rearrange("p t (c i) -> p c t i", i=4),
+                out=grouped[:].rearrange("p (c i t) -> p c t i", i=NEIGHBOURS, t=PACK),
+                in_=raw[:].rearrange("p t (c i) -> p c t i", i=NEIGHBOURS),
             )
             quantize(operand, cols, grouped[:], fmt)
 
@@ -97,7 +102,7 @@ def tile_attend_glstm_u_kernel(tc, wo, dy, dcn, gi, gf, go, gc, ct, cp, h0, offs
             words = dealt_bf16[:].bitcast(F32)
             count = dealt_bf16.shape[1] // WIDTH
             for n in range(2 * count):
-                nc.tensor.transpose(bank[:, n, :], words[:, blocks(n)], ident[:])
+                nc.tensor.transpose(bank[:, n, :], words[:, strips(n)], ident[:])
             copy(
                 out=grouped.bitcast(F32).rearrange("p (g c u) -> p g c u", g=count, u=2),
                 in_=bank[:, : 2 * count, :].rearrange("p (g u) c -> p g c u", u=2),
@@ -129,7 +134,7 @@ def tile_attend_glstm_u_kernel(tc, wo, dy, dcn, gi, gf, go, gc, ct, cp, h0, offs
             factors[gate, j] = factor
 
         def times_dh(j):
-            dh = product(wo_q, blocks(j), E4M3X4, dy_q, blocks(0, TILES), E5M2X4)
+            dh = product(wo_q, strips(j), E4M3X4, dy_q, strips(0, TILES), E5M2X4)
             through = factors["o", j]
             nc.vector.tensor_tensor(out=through[:], in0=through[:], in1=dh[:], op=MULT)
 
@@ -150,14 +155,14 @@ def tile_attend_glstm_u_kernel(tc, wo, dy, dcn, gi, gf, go, gc, ct, cp, h0, offs
                 )
             return z
 
-        def grouped_blocks(grouped, first, count):
+        def grouped_strips(grouped, first, count):
             return grouped[:, first * WIDTH : (first + count) * WIDTH]
 
         def turn_z(z, first, bank, copy):
-            turn(z, grouped_blocks(z_grouped, first, z.shape[1] // WIDTH), bank, copy)
+            turn(z, grouped_strips(z_grouped, first, z.shape[1] // WIDTH), bank, copy)
 
         def quantize_z(first, count):
-            quantize(z_q, blocks(first, count), grouped_blocks(z_grouped, first, count), E5M2X4)
+            quantize(z_q, strips(first, count), grouped_strips(z_grouped, first, count), E5M2X4)
 
         def old_hidden(k):
             rows = load_rows(h0, k)
@@ -165,44 +170,44 @@ def tile_attend_glstm_u_kernel(tc, wo, dy, dcn, gi, gf, go, gc, ct, cp, h0, offs
             nc.scalar.activation(out=rows_bf16[:], in_=rows[:], func=COPY)
             picked = work.tile([P, WIDTH], BF16, name="h0_picked", align_bytes=64)
             nc.scalar.activation(out=dealt(picked[:]), in_=listed(rows_bf16), func=COPY)
-            turn(picked, grouped_blocks(h0_grouped, k, 1), turn_bank, nc.scalar.copy)
+            turn(picked, grouped_strips(h0_grouped, k, 1), turn_bank, nc.scalar.copy)
 
         def store(out, first, count, cols, staged):
-            nc.sync.dma_start(out=out[blocks(first, count), cols].rearrange("(k p) h -> p k h", p=P), in_=staged)
+            nc.sync.dma_start(out=out[strips(first, count), cols].rearrange("(k p) h -> p k h", p=P), in_=staged)
 
         def outputs_of_tile_0():
             for g, out in enumerate((out_0, out_1)):
-                acc = product(z_q, blocks(g), E5M2X4, h0_q, blocks(0, TILES), E4M3X4)
+                acc = product(z_q, strips(g), E5M2X4, h0_q, strips(0, TILES), E4M3X4)
                 by_h = work.tile([P, WIDTH], F32, name="by_h")
                 nc.scalar.copy(out=by_h[:], in_=acc[:])
-                back = psum.tile([P, TILES, P], F32, name="acc", bufs=6)
+                back = psum.tile([P, TILES, P], F32, name="acc", bufs=ACC_BANKS)
                 for k in range(TILES):
-                    nc.tensor.transpose(back[:, k, :], by_h[:, blocks(k)], ident[:])
+                    nc.tensor.transpose(back[:, k, :], by_h[:, strips(k)], ident[:])
                 staged = work.tile([P, TILES, P], F32, name="staged_0")
                 nc.scalar.copy(out=staged[:], in_=back[:])
-                store(out, 0, TILES, blocks(0), staged[:])
+                store(out, 0, TILES, strips(0), staged[:])
 
         def outputs_of_tiles_1_2():
             staged = work.tile([P, TILES, WIDTH], F32, name="staged_1_2", tag="raw")
             for k in range(TILES):
-                acc = product(h0_q, blocks(k), E4M3X4, z_q, blocks(2, 4), E5M2X4)
+                acc = product(h0_q, strips(k), E4M3X4, z_q, strips(2, 4), E5M2X4)
                 nc.scalar.copy(
                     out=staged[:, k, :].rearrange("p (g j c) -> p g j c", g=2, j=2),
                     in_=acc[:].rearrange("p (j g c) -> p g j c", g=2, j=2),
                 )
                 if k % 2 == 1:
                     for g, out in enumerate((out_0, out_1)):
-                        store(out, k - 1, 2, blocks(1, 2), staged[:, k - 1 : k + 1, blocks(2 * g, 2)])
+                        store(out, k - 1, 2, strips(1, 2), staged[:, k - 1 : k + 1, strips(2 * g, 2)])
 
         def outputs_of_tile_3():
             staged = work.tile([P, TILES, 2 * P], F32, name="staged_3", tag="raw")
             for k in range(TILES):
-                acc = product(h0_q, blocks(k), E4M3X4, z_q, blocks(4, 4), E5M2X4)
+                acc = product(h0_q, strips(k), E4M3X4, z_q, strips(4, 4), E5M2X4)
                 copy = nc.vector.tensor_copy if k % 2 else nc.scalar.copy
-                copy(out=staged[:, k, :], in_=acc[:, blocks(2, 2)])
+                copy(out=staged[:, k, :], in_=acc[:, strips(2, 2)])
                 if k % 2 == 1:
                     for g, out in enumerate((out_0, out_1)):
-                        store(out, k - 1, 2, blocks(3), staged[:, k - 1 : k + 1, blocks(g)])
+                        store(out, k - 1, 2, strips(3), staged[:, k - 1 : k + 1, strips(g)])
 
         first_rows = load_rows(gi, 0)
         nc.sync.dma_start(out=offsets[:], in_=offs)
@@ -211,15 +216,17 @@ def tile_attend_glstm_u_kernel(tc, wo, dy, dcn, gi, gf, go, gc, ct, cp, h0, offs
             slopes["f", j] = gate_slope(load_rows(gf, j))
         for j in range(TILES):
             slopes["o", j] = tanh_slope(load_rows(ct, j))
+
         for gate in "ifo":
             make_factor(gate, 0)
-        quantize_along_m(dy, dy_q, blocks(0, TILES), E5M2X4, "raw")
+        quantize_along_m(dy, dy_q, strips(0, TILES), E5M2X4, "raw")
         make_factor("i", 1)
-        quantize_along_m(wo, wo_q, blocks(0, 2), E4M3X4, "wo_raw")
+        quantize_along_m(wo, wo_q, strips(0, 2), E4M3X4, "wo_raw")
         make_factor("f", 1)
         make_factor("o", 1)
         times_dh(0)
         times_dh(1)
+
         old_hidden(0)
         z0 = gate_gradients(cell_gradient(0), 0, "if")
         old_hidden(1)
@@ -227,20 +234,22 @@ def tile_attend_glstm_u_kernel(tc, wo, dy, dcn, gi, gf, go, gc, ct, cp, h0, offs
         z1 = gate_gradients(cell_gradient(1), 1, "if")
         old_hidden(2)
         make_factor("o", 2)
-        quantize_along_m(wo, wo_q, blocks(2, 2), E4M3X4, "wo_raw")
+        quantize_along_m(wo, wo_q, strips(2, 2), E4M3X4, "wo_raw")
         make_factor("o", 3)
         make_factor("i", 2)
         times_dh(2)
         times_dh(3)
         old_hidden(3)
-        quantize(h0_q, blocks(0, TILES), h0_grouped[:], E4M3X4)
+        quantize(h0_q, strips(0, TILES), h0_grouped[:], E4M3X4)
         quantize_z(0, 2)
         turn_z(z1, 2, turn_bank, nc.scalar.copy)
+
         make_factor("f", 2)
         turn_z(gate_gradients(cell_gradient(2), 2, "if"), 4, turn_bank, nc.scalar.copy)
         quantize_z(2, 4)
         outputs_of_tile_0()
         outputs_of_tiles_1_2()
+
         make_factor("i", 3)
         make_factor("f", 3)
         dc = cell_gradient(3)
@@ -248,4 +257,5 @@ def tile_attend_glstm_u_kernel(tc, wo, dy, dcn, gi, gf, go, gc, ct, cp, h0, offs
         quantize_z(6, 1)
         turn_z(gate_gradients(dc, 3, "f"), 7, last_bank, nc.vector.tensor_copy)
         quantize_z(7, 1)
+        product(h0_q, strips(0), E4M3X4, z_q, strips(2, 4), E5M2X4, turn_bank[:].rearrange("p n c -> p (n c)"))
         outputs_of_tile_3()

@@ -63,9 +63,6 @@ def tile_attend_glstm_u_kernel(tc, wo, dy, dcn, gi, gf, go, gc, ct, cp, h0, offs
         def listed(window):
             return window[:].indirect(offsets[:])
 
-        def in_order(ap):
-            return ap.rearrange("p (b u x) -> p b u x", u=2, x=RUN)
-
         def dealt(ap):
             return ap.rearrange("p (u b x) -> p b u x", u=2, x=RUN)
 
@@ -105,7 +102,7 @@ def tile_attend_glstm_u_kernel(tc, wo, dy, dcn, gi, gf, go, gc, ct, cp, h0, offs
                 nc.tensor.transpose(bank[:, n, :], words[:, strips(n)], ident[:])
             copy(
                 out=grouped.bitcast(F32).rearrange("p (g c u) -> p g c u", g=count, u=2),
-                in_=bank[:, : 2 * count, :].rearrange("p (g u) c -> p g c u", u=2),
+                in_=bank[:, : 2 * count, :].rearrange("p (u g) c -> p g c u", u=2),
             )
 
         def gate_slope(rows):
@@ -126,33 +123,41 @@ def tile_attend_glstm_u_kernel(tc, wo, dy, dcn, gi, gf, go, gc, ct, cp, h0, offs
         partner = {"i": gc, "f": cp, "o": go}
         slopes = {}
         factors = {}
+        pairs = [keep.tile([P, 2, WIDTH], F32, name="factors_%d" % j) for j in range(TILES)]
 
         def make_factor(gate, j):
             rows = load_rows(partner[gate], j)
-            factor = work.tile([P, WIDTH], F32, name="factor", bufs=3 * TILES)
-            nc.vector.tensor_tensor(out=factor[:], in0=listed(rows), in1=slopes[gate, j][:], op=MULT)
+            if gate == "o":
+                factor = work.tile([P, WIDTH], F32, name="factor_o", bufs=TILES)[:]
+            else:
+                factor = pairs[j][:, "if".index(gate), :]
+            nc.vector.tensor_tensor(out=factor, in0=listed(rows), in1=slopes[gate, j][:], op=MULT)
             factors[gate, j] = factor
 
         def times_dh(j):
             dh = product(wo_q, strips(j), E4M3X4, dy_q, strips(0, TILES), E5M2X4)
             through = factors["o", j]
-            nc.vector.tensor_tensor(out=through[:], in0=through[:], in1=dh[:], op=MULT)
+            nc.vector.tensor_tensor(out=through, in0=through, in1=dh[:], op=MULT)
 
         def cell_gradient(j):
             rows = load_rows(dcn, j)
             dc = work.tile([P, WIDTH], F32, name="dc")
-            nc.vector.tensor_tensor(out=dc[:], in0=listed(rows), in1=factors["o", j][:], op=ADD)
+            nc.vector.tensor_tensor(out=dc[:], in0=listed(rows), in1=factors["o", j], op=ADD)
             return dc
 
         def gate_gradients(dc, j, gates):
-            z = work.tile([P, len(gates) * WIDTH], BF16, name="z", bufs=4, align_bytes=64)
-            for n, gate in enumerate(gates):
-                nc.vector.tensor_tensor(
-                    out=dealt(z[:, n * WIDTH : (n + 1) * WIDTH]),
-                    in0=in_order(factors[gate, j][:]),
-                    in1=in_order(dc[:]),
-                    op=MULT,
-                )
+            count = len(gates)
+            first = "if".index(gates[0])
+            z = work.tile([P, count * WIDTH], BF16, name="z", bufs=4, align_bytes=64)
+            nc.vector.tensor_tensor(
+                out=z[:].rearrange("p (u g b x) -> p g b u x", u=2, g=count, x=RUN),
+                in0=pairs[j][:, first : first + count, :].rearrange("p g (b u x) -> p g b u x", u=2, x=RUN),
+                in1=dc[:]
+                .unsqueeze(1)
+                .to_broadcast([P, count, WIDTH])
+                .rearrange("p g (b u x) -> p g b u x", u=2, x=RUN),
+                op=MULT,
+            )
             return z
 
         def grouped_strips(grouped, first, count):
@@ -205,9 +210,10 @@ def tile_attend_glstm_u_kernel(tc, wo, dy, dcn, gi, gf, go, gc, ct, cp, h0, offs
                 acc = product(h0_q, strips(k), E4M3X4, z_q, strips(4, 4), E5M2X4)
                 copy = nc.vector.tensor_copy if k % 2 else nc.scalar.copy
                 copy(out=staged[:, k, :], in_=acc[:, strips(2, 2)])
-                if k % 2 == 1:
+                if k != 1:
+                    first = 1 if k == 2 else k
                     for g, out in enumerate((out_0, out_1)):
-                        store(out, k - 1, 2, strips(3), staged[:, k - 1 : k + 1, strips(g)])
+                        store(out, first, k + 1 - first, strips(3), staged[:, first : k + 1, strips(g)])
 
         first_rows = load_rows(gi, 0)
         nc.sync.dma_start(out=offsets[:], in_=offs)

@@ -55,9 +55,9 @@ def tile_attend_glstm_u_kernel(tc, wo, dy, dcn, gi, gf, go, gc, ct, cp, h0, offs
         def strips(first, count=1):
             return slice(first * P, (first + count) * P)
 
-        def load_rows(table, j):
+        def load_rows(table, j, queue=nc.sync):
             window = work.tile([P, SESSIONS], F32, name="window", bufs=WINDOWS)
-            nc.sync.dma_start(out=window[:], in_=table[strips(j), :])
+            queue.dma_start(out=window[:], in_=table[strips(j), :])
             return window
 
         def listed(window):
@@ -219,7 +219,7 @@ def tile_attend_glstm_u_kernel(tc, wo, dy, dcn, gi, gf, go, gc, ct, cp, h0, offs
         nc.sync.dma_start(out=offsets[:], in_=offs)
         for j in range(TILES):
             slopes["i", j] = gate_slope(first_rows if j == 0 else load_rows(gi, j))
-            slopes["f", j] = gate_slope(load_rows(gf, j))
+            slopes["f", j] = gate_slope(load_rows(gf, j, nc.scalar))
         for j in range(TILES):
             slopes["o", j] = tanh_slope(load_rows(ct, j))
 

@@ -11,7 +11,7 @@ U8 = mybir.dt.uint8
 E4M3X4 = mybir.dt.float8_e4m3fn_x4
 E5M2X4 = mybir.dt.float8_e5m2_x4
 MULT = mybir.AluOpType.mult
-ADD = mybir.AluOpType.add
+SUBTRACT = mybir.AluOpType.subtract
 COPY = mybir.ActivationFunctionType.Copy
 SQUARE = mybir.ActivationFunctionType.Square
 
@@ -20,10 +20,10 @@ PACK = 4
 WIDTH = 512
 SESSIONS = 1024
 TILES = WIDTH // P
-RUN = 16
 NEIGHBOURS = 4
 WINDOWS = 24
 ACC_BANKS = 6
+TURN_BANKS = 2
 FLOPS = 3 * 2 * WIDTH * WIDTH * WIDTH
 
 
@@ -46,222 +46,180 @@ def tile_attend_glstm_u_kernel(tc, wo, dy, dcn, gi, gf, go, gc, ct, cp, h0, offs
         wo_q = quantized("wo", WIDTH)
         dy_q = quantized("dy", WIDTH)
         h0_q = quantized("h0", WIDTH)
-        z_q = quantized("z", 2 * WIDTH)
-        h0_grouped = keep.tile([P, WIDTH * PACK], BF16, name="h0_grouped", align_bytes=64)
-        z_grouped = keep.tile([P, 2 * WIDTH * PACK], BF16, name="z_grouped", align_bytes=64)
-        turn_bank = psum.tile([P, 4, P], F32, name="turn_bank")
-        last_bank = psum.tile([P, 2, P], F32, name="last_bank")
+        z_q = [quantized("zi", WIDTH), quantized("zf", WIDTH)]
 
-        def strips(first, count=1):
-            return slice(first * P, (first + count) * P)
+        def strip(j):
+            return slice(j * P, (j + 1) * P)
 
-        def load_rows(table, j, queue=nc.sync):
-            window = work.tile([P, SESSIONS], F32, name="window", bufs=WINDOWS)
-            queue.dma_start(out=window[:], in_=table[strips(j), :])
+        whole = slice(0, WIDTH)
+
+        def load_rows(table, j, tag="window"):
+            window = work.tile([P, SESSIONS], F32, name="window", tag=tag, bufs=WINDOWS if tag == "window" else 1)
+            nc.sync.dma_start(out=window[:], in_=table[strip(j), :])
             return window
 
         def listed(window):
             return window[:].indirect(offsets[:])
 
-        def dealt(ap):
-            return ap.rearrange("p (u b x) -> p b u x", u=2, x=RUN)
-
         def quantize(operand, cols, grouped, fmt):
             codes, scales = operand
             nc.vector.quantize_mx(out=codes[:, cols].bitcast(fmt), scales=scales[:, cols], in_=grouped)
 
-        def product(lhs, lhs_cols, lhs_fmt, rhs, rhs_cols, rhs_fmt, acc=None):
-            if acc is None:
-                acc = psum.tile([P, WIDTH], F32, name="acc", bufs=ACC_BANKS)
+        def product(acc, lhs, lhs_cols, rhs, rhs_cols):
             nc.tensor.matmul_mx(
-                out=acc[:],
-                lhsT=lhs[0][:, lhs_cols].bitcast(lhs_fmt),
+                out=acc,
+                lhsT=lhs[0][:, lhs_cols].bitcast(E4M3X4),
                 lhsT_scale=lhs[1][:, lhs_cols],
-                rhs=rhs[0][:, rhs_cols].bitcast(rhs_fmt),
+                rhs=rhs[0][:, rhs_cols].bitcast(E5M2X4),
                 rhs_scale=rhs[1][:, rhs_cols],
                 start=True,
                 stop=True,
             )
-            return acc
 
-        def quantize_along_m(src, operand, cols, fmt, tag):
-            columns = cols.stop - cols.start
-            raw = work.tile([P, PACK, columns], F32, name="raw", tag=tag)
-            nc.sync.dma_start(out=raw[:], in_=src[:, cols].rearrange("(p t) c -> p t c", t=PACK))
-            grouped = work.tile([P, columns * PACK], BF16, name="grouped_m", bufs=3, align_bytes=64)
-            nc.scalar.copy(
+        def bank():
+            return psum.tile([P, WIDTH], F32, name="acc", bufs=ACC_BANKS)
+
+        def quantize_along_m(src, operand, fmt):
+            raw = work.tile([P, PACK, WIDTH], F32, name="raw")
+            nc.sync.dma_start(out=raw[:], in_=src.rearrange("(p t) c -> p t c", t=PACK))
+            grouped = work.tile([P, WIDTH * PACK], BF16, name="grouped_m", align_bytes=64)
+            nc.vector.tensor_copy(
                 out=grouped[:].rearrange("p (c i t) -> p c t i", i=NEIGHBOURS, t=PACK),
                 in_=raw[:].rearrange("p t (c i) -> p c t i", i=NEIGHBOURS),
             )
-            quantize(operand, cols, grouped[:], fmt)
+            quantize(operand, whole, grouped[:], fmt)
 
-        def turn(dealt_bf16, grouped, bank, copy):
-            words = dealt_bf16[:].bitcast(F32)
-            count = dealt_bf16.shape[1] // WIDTH
-            for n in range(2 * count):
-                nc.tensor.transpose(bank[:, n, :], words[:, strips(n)], ident[:])
+        def turn(rows_bf16, count, copy):
+            words = rows_bf16[:].bitcast(F32).rearrange("p (g w u) -> p g u w", g=count, u=2)
+            bank = psum.tile([P, 2, 2, P], F32, name="turn_bank", bufs=TURN_BANKS)
+            for g in range(count):
+                for u in range(2):
+                    nc.tensor.transpose(bank[:, g, u, :], words[:, g, u, :], ident[:])
+            grouped = work.tile([P, count, WIDTH], BF16, name="grouped_%d" % count, align_bytes=64)
             copy(
-                out=grouped.bitcast(F32).rearrange("p (g c u) -> p g c u", g=count, u=2),
-                in_=bank[:, : 2 * count, :].rearrange("p (u g) c -> p g c u", u=2),
+                out=grouped[:].bitcast(F32).rearrange("p g (c u) -> p g c u", u=2),
+                in_=bank[:, :count, :, :].rearrange("p g u c -> p g c u"),
             )
+            return grouped
 
-        def gate_slope(rows):
-            gate = work.tile([P, WIDTH], F32, name="gate", bufs=3)
-            nc.vector.tensor_copy(out=gate[:], in_=listed(rows))
-            slope = work.tile([P, WIDTH], F32, name="slope", bufs=3 * TILES)
-            nc.scalar.activation(out=slope[:], in_=gate[:], func=COPY, scale=-1.0, bias=1.0)
-            nc.gpsimd.tensor_tensor(out=slope[:], in0=gate[:], in1=slope[:], op=MULT)
-            return slope
+        def picked(table, j, out, tag="window"):
+            nc.scalar.activation(out=out, in_=listed(load_rows(table, j, tag)), func=COPY)
 
-        def tanh_slope(rows):
-            slope = work.tile([P, WIDTH], F32, name="slope", bufs=3 * TILES)
-            nc.vector.tensor_copy(out=slope[:], in_=listed(rows))
-            nc.scalar.activation(out=slope[:], in_=slope[:], func=SQUARE)
-            nc.scalar.activation(out=slope[:], in_=slope[:], func=COPY, scale=-1.0, bias=1.0)
-            return slope
+        def picked_times(table, j, other, out):
+            nc.vector.tensor_tensor(out=out, in0=listed(load_rows(table, j)), in1=other, op=MULT)
 
-        partner = {"i": gc, "f": cp, "o": go}
-        slopes = {}
-        factors = {}
-        pairs = [keep.tile([P, 2, WIDTH], F32, name="factors_%d" % j) for j in range(TILES)]
+        def row(name):
+            return work.tile([P, WIDTH], F32, name=name)
 
-        def make_factor(gate, j):
-            rows = load_rows(partner[gate], j)
-            if gate == "o":
-                factor = work.tile([P, WIDTH], F32, name="factor_o", bufs=TILES)[:]
-            else:
-                factor = pairs[j][:, "if".index(gate), :]
-            nc.vector.tensor_tensor(out=factor, in0=listed(rows), in1=slopes[gate, j][:], op=MULT)
-            factors[gate, j] = factor
+        def minus_one_times(out, in0, in1):
+            nc.vector.scalar_tensor_tensor(out=out, in0=in0, scalar=1.0, in1=in1, op0=SUBTRACT, op1=MULT)
 
-        def times_dh(j):
-            dh = product(wo_q, strips(j), E4M3X4, dy_q, strips(0, TILES), E5M2X4)
-            through = factors["o", j]
-            nc.vector.tensor_tensor(out=through, in0=through, in1=dh[:], op=MULT)
+        def through_tanh(j):
+            tanh_c = row("tanh_c")
+            through = row("through")
+            picked(ct, j, tanh_c[:])
+            nc.scalar.activation(out=tanh_c[:], in_=tanh_c[:], func=SQUARE)
+            minus_one_times(through[:], tanh_c[:], dh[j][:])
+            return through
 
-        def cell_gradient(j):
-            rows = load_rows(dcn, j)
-            dc = work.tile([P, WIDTH], F32, name="dc")
-            nc.vector.tensor_tensor(out=dc[:], in0=listed(rows), in1=factors["o", j], op=ADD)
-            return dc
+        def subtract_incoming(j, minus_dc):
+            incoming = row("incoming")
+            picked(dcn, j, incoming[:])
+            nc.vector.tensor_tensor(out=minus_dc[:], in0=minus_dc[:], in1=incoming[:], op=SUBTRACT)
 
-        def gate_gradients(dc, j, gates):
-            count = len(gates)
-            first = "if".index(gates[0])
-            z = work.tile([P, count * WIDTH], BF16, name="z", bufs=4, align_bytes=64)
+        def gradients(j, first, count, factors, minus_dc):
+            z = work.tile([P, count * WIDTH], BF16, name="z", align_bytes=64)
             nc.vector.tensor_tensor(
-                out=z[:].rearrange("p (u g b x) -> p g b u x", u=2, g=count, x=RUN),
-                in0=pairs[j][:, first : first + count, :].rearrange("p g (b u x) -> p g b u x", u=2, x=RUN),
-                in1=dc[:]
-                .unsqueeze(1)
-                .to_broadcast([P, count, WIDTH])
-                .rearrange("p g (b u x) -> p g b u x", u=2, x=RUN),
+                out=z[:].rearrange("p (g i) -> p g i", g=count),
+                in0=factors[:, first : first + count, :],
+                in1=minus_dc[:].unsqueeze(1).to_broadcast([P, count, WIDTH]),
                 op=MULT,
             )
-            return z
-
-        def grouped_strips(grouped, first, count):
-            return grouped[:, first * WIDTH : (first + count) * WIDTH]
-
-        def turn_z(z, first, bank, copy):
-            turn(z, grouped_strips(z_grouped, first, z.shape[1] // WIDTH), bank, copy)
-
-        def quantize_z(first, count):
-            quantize(z_q, strips(first, count), grouped_strips(z_grouped, first, count), E5M2X4)
+            grouped = turn(z, count, nc.vector.tensor_copy)
+            for g in range(count):
+                quantize(z_q[first + g], strip(j), grouped[:, g, :], E5M2X4)
 
         def old_hidden(k):
-            rows = load_rows(h0, k)
-            rows_bf16 = work.tile([P, SESSIONS], BF16, name="h0_bf16")
-            nc.scalar.activation(out=rows_bf16[:], in_=rows[:], func=COPY)
-            picked = work.tile([P, WIDTH], BF16, name="h0_picked", align_bytes=64)
-            nc.scalar.activation(out=dealt(picked[:]), in_=listed(rows_bf16), func=COPY)
-            turn(picked, grouped_strips(h0_grouped, k, 1), turn_bank, nc.scalar.copy)
+            rows = work.tile([P, WIDTH], BF16, name="old_hidden", align_bytes=64)
+            picked(h0, k, rows[:])
+            grouped = turn(rows, 1, nc.scalar.copy)
+            quantize(h0_q, strip(k), grouped[:, 0, :], E4M3X4)
 
-        def store(out, first, count, cols, staged):
-            nc.sync.dma_start(out=out[strips(first, count), cols].rearrange("(k p) h -> p k h", p=P), in_=staged)
+        def ordinary_tile(j):
+            gates = work.tile([P, 2, WIDTH], F32, name="gates")
+            factors = work.tile([P, 2, WIDTH], F32, name="factors")
+            minus_dc = row("minus_dc")
+            through = through_tanh(j)
+            if j > 0:
+                old_hidden(j)
+            picked(gi, j, gates[:, 0, :])
+            picked_times(gc, j, gates[:, 0, :], factors[:, 0, :])
+            picked(go, j, minus_dc[:])
+            nc.vector.tensor_tensor(out=minus_dc[:], in0=minus_dc[:], in1=through[:], op=MULT)
+            picked(gf, j, gates[:, 1, :])
+            picked_times(cp, j, gates[:, 1, :], factors[:, 1, :])
+            minus_one_times(factors[:], gates[:], factors[:])
+            subtract_incoming(j, minus_dc)
+            gradients(j, 0, 2, factors, minus_dc)
 
-        def outputs_of_tile_0():
-            for g, out in enumerate((out_0, out_1)):
-                acc = product(z_q, strips(g), E5M2X4, h0_q, strips(0, TILES), E4M3X4)
-                by_h = work.tile([P, WIDTH], F32, name="by_h")
-                nc.scalar.copy(out=by_h[:], in_=acc[:])
-                back = psum.tile([P, TILES, P], F32, name="acc", bufs=ACC_BANKS)
-                for k in range(TILES):
-                    nc.tensor.transpose(back[:, k, :], by_h[:, strips(k)], ident[:])
-                staged = work.tile([P, TILES, P], F32, name="staged_0")
-                nc.scalar.copy(out=staged[:], in_=back[:])
-                store(out, 0, TILES, strips(0), staged[:])
+        def whole_rows(g, k, copy):
+            acc = bank()
+            product(acc[:], h0_q, strip(k), z_q[g], whole)
+            staged = work.tile([P, WIDTH], F32, name="staged", bufs=TILES + 1)
+            copy(out=staged[:], in_=acc[:])
+            nc.sync.dma_start(out=outs[g][strip(k), :], in_=staged[:])
 
-        def outputs_of_tiles_1_2():
-            staged = work.tile([P, TILES, WIDTH], F32, name="staged_1_2", tag="raw")
-            for k in range(TILES):
-                acc = product(h0_q, strips(k), E4M3X4, z_q, strips(2, 4), E5M2X4)
-                nc.scalar.copy(
-                    out=staged[:, k, :].rearrange("p (g j c) -> p g j c", g=2, j=2),
-                    in_=acc[:].rearrange("p (j g c) -> p g j c", g=2, j=2),
-                )
-                if k % 2 == 1:
-                    for g, out in enumerate((out_0, out_1)):
-                        store(out, k - 1, 2, strips(1, 2), staged[:, k - 1 : k + 1, strips(2 * g, 2)])
+        last = TILES - 1
+        early = last * P
 
-        def outputs_of_tile_3():
-            staged = work.tile([P, TILES, 2 * P], F32, name="staged_3", tag="raw")
-            for k in range(TILES):
-                acc = product(h0_q, strips(k), E4M3X4, z_q, strips(4, 4), E5M2X4)
-                copy = nc.vector.tensor_copy if k % 2 else nc.scalar.copy
-                copy(out=staged[:, k, :], in_=acc[:, strips(2, 2)])
-                if k != 1:
-                    first = 1 if k == 2 else k
-                    for g, out in enumerate((out_0, out_1)):
-                        store(out, first, k + 1 - first, strips(3), staged[:, first : k + 1, strips(g)])
+        def early_columns(g):
+            staged = work.tile([P, last, early], F32, name="staged_early", tag="late", bufs=1)
+            for k in range(last):
+                acc = bank()
+                product(acc[:, : 2 * P], h0_q, strip(k), z_q[g], slice(0, 2 * P))
+                product(acc[:, strip(2)], h0_q, strip(k), z_q[g], strip(2))
+                nc.scalar.copy(out=staged[:, k, :], in_=acc[:, :early])
+            nc.sync.dma_start(out=outs[g][:early, :early].rearrange("(k p) h -> p k h", p=P), in_=staged[:])
 
-        first_rows = load_rows(gi, 0)
+        def late_columns(g, copy):
+            acc = bank()
+            for k in range(last):
+                product(acc[:, strip(k)], h0_q, strip(k), z_q[g], strip(last))
+            staged = work.tile([P, last, P], F32, name="staged_late", bufs=1)
+            copy(out=staged[:], in_=acc[:, :early].rearrange("p (k h) -> p k h", k=last))
+            nc.sync.dma_start(out=outs[g][:early, strip(last)].rearrange("(k p) h -> p k h", p=P), in_=staged[:])
+
+        def last_tile(j):
+            gates = work.tile([P, 2, WIDTH], F32, name="gates")
+            factors = work.tile([P, 2, WIDTH], F32, name="factors")
+            minus_dc = row("minus_dc")
+            through = through_tanh(j)
+            picked(gi, j, gates[:, 0, :])
+            picked_times(gc, j, gates[:, 0, :], factors[:, 0, :])
+            picked(gf, j, gates[:, 1, :])
+            picked_times(cp, j, gates[:, 1, :], factors[:, 1, :])
+            minus_one_times(factors[:], gates[:], factors[:])
+            picked(go, j, minus_dc[:], "late")
+            nc.vector.tensor_tensor(out=minus_dc[:], in0=minus_dc[:], in1=through[:], op=MULT)
+            subtract_incoming(j, minus_dc)
+            gradients(j, 0, 1, factors, minus_dc)
+            gradients(j, 1, 1, factors, minus_dc)
+            old_hidden(j)
+            early_columns(1)
+            for k in range(last):
+                whole_rows(0, k, nc.scalar.copy)
+            whole_rows(0, last, nc.vector.tensor_copy)
+            whole_rows(1, last, nc.scalar.copy)
+            late_columns(1, nc.vector.tensor_copy)
+
+        outs = (out_0, out_1)
         nc.sync.dma_start(out=offsets[:], in_=offs)
-        for j in range(TILES):
-            slopes["i", j] = gate_slope(first_rows if j == 0 else load_rows(gi, j))
-            slopes["f", j] = gate_slope(load_rows(gf, j, nc.scalar))
-        for j in range(TILES):
-            slopes["o", j] = tanh_slope(load_rows(ct, j))
-
-        for gate in "ifo":
-            make_factor(gate, 0)
-        quantize_along_m(dy, dy_q, strips(0, TILES), E5M2X4, "raw")
-        make_factor("i", 1)
-        quantize_along_m(wo, wo_q, strips(0, 2), E4M3X4, "wo_raw")
-        make_factor("f", 1)
-        make_factor("o", 1)
-        times_dh(0)
-        times_dh(1)
-
         old_hidden(0)
-        z0 = gate_gradients(cell_gradient(0), 0, "if")
-        old_hidden(1)
-        turn_z(z0, 0, turn_bank, nc.scalar.copy)
-        z1 = gate_gradients(cell_gradient(1), 1, "if")
-        old_hidden(2)
-        make_factor("o", 2)
-        quantize_along_m(wo, wo_q, strips(2, 2), E4M3X4, "wo_raw")
-        make_factor("o", 3)
-        make_factor("i", 2)
-        times_dh(2)
-        times_dh(3)
-        old_hidden(3)
-        quantize(h0_q, strips(0, TILES), h0_grouped[:], E4M3X4)
-        quantize_z(0, 2)
-        turn_z(z1, 2, turn_bank, nc.scalar.copy)
-
-        make_factor("f", 2)
-        turn_z(gate_gradients(cell_gradient(2), 2, "if"), 4, turn_bank, nc.scalar.copy)
-        quantize_z(2, 4)
-        outputs_of_tile_0()
-        outputs_of_tiles_1_2()
-
-        make_factor("i", 3)
-        make_factor("f", 3)
-        dc = cell_gradient(3)
-        turn_z(gate_gradients(dc, 3, "i"), 6, turn_bank, nc.vector.tensor_copy)
-        quantize_z(6, 1)
-        turn_z(gate_gradients(dc, 3, "f"), 7, last_bank, nc.vector.tensor_copy)
-        quantize_z(7, 1)
-        product(h0_q, strips(0), E4M3X4, z_q, strips(2, 4), E5M2X4, turn_bank[:].rearrange("p n c -> p (n c)"))
-        outputs_of_tile_3()
+        quantize_along_m(dy, dy_q, E5M2X4)
+        quantize_along_m(wo, wo_q, E4M3X4)
+        dh = [bank() for j in range(TILES)]
+        for j in range(TILES):
+            product(dh[j][:], wo_q, strip(j), dy_q, whole)
+        for j in range(last):
+            ordinary_tile(j)
+        last_tile(last)

@@ -21,7 +21,7 @@ WIDTH = 512
 SESSIONS = 1024
 TILES = WIDTH // P
 NEIGHBOURS = 4
-WINDOWS = 24
+WINDOWS = 22
 ACC_BANKS = 6
 TURN_BANKS = 2
 FLOPS = 3 * 2 * WIDTH * WIDTH * WIDTH
@@ -53,8 +53,11 @@ def tile_attend_glstm_u_kernel(tc, wo, dy, dcn, gi, gf, go, gc, ct, cp, h0, offs
 
         whole = slice(0, WIDTH)
 
-        def load_rows(table, j, tag="window"):
-            window = work.tile([P, SESSIONS], F32, name="window", tag=tag, bufs=WINDOWS if tag == "window" else 1)
+        def load_rows(table, j, tag=None):
+            if tag is None:
+                window = work.tile([P, SESSIONS], F32, name="window", bufs=WINDOWS)
+            else:
+                window = keep.tile([P, SESSIONS], F32, name="window", tag=tag, align_bytes=64)
             nc.sync.dma_start(out=window[:], in_=table[strip(j), :])
             return window
 
@@ -89,20 +92,23 @@ def tile_attend_glstm_u_kernel(tc, wo, dy, dcn, gi, gf, go, gc, ct, cp, h0, offs
             )
             quantize(operand, whole, grouped[:], fmt)
 
-        def turn(rows_bf16, count, copy):
+        def turn(rows_bf16, count, copy, tag=None):
             words = rows_bf16[:].bitcast(F32).rearrange("p (g w u) -> p g u w", g=count, u=2)
             bank = psum.tile([P, 2, 2, P], F32, name="turn_bank", bufs=TURN_BANKS)
             for g in range(count):
                 for u in range(2):
                     nc.tensor.transpose(bank[:, g, u, :], words[:, g, u, :], ident[:])
-            grouped = work.tile([P, count, WIDTH], BF16, name="grouped_%d" % count, align_bytes=64)
+            if tag is None:
+                grouped = work.tile([P, count, WIDTH], BF16, name="grouped_%d" % count, align_bytes=64)
+            else:
+                grouped = keep.tile([P, count, WIDTH], BF16, name="grouped", tag=tag, align_bytes=64)
             copy(
                 out=grouped[:].bitcast(F32).rearrange("p g (c u) -> p g c u", u=2),
                 in_=bank[:, :count, :, :].rearrange("p g u c -> p g c u"),
             )
             return grouped
 
-        def picked(table, j, out, tag="window"):
+        def picked(table, j, out, tag=None):
             nc.scalar.activation(out=out, in_=listed(load_rows(table, j, tag)), func=COPY)
 
         def picked_times(table, j, other, out):
@@ -114,28 +120,24 @@ def tile_attend_glstm_u_kernel(tc, wo, dy, dcn, gi, gf, go, gc, ct, cp, h0, offs
         def minus_one_times(out, in0, in1):
             nc.vector.scalar_tensor_tensor(out=out, in0=in0, scalar=1.0, in1=in1, op0=SUBTRACT, op1=MULT)
 
-        def through_tanh(j):
+        def tanh_squared(j):
             tanh_c = row("tanh_c")
-            through = row("through")
             picked(ct, j, tanh_c[:])
             nc.scalar.activation(out=tanh_c[:], in_=tanh_c[:], func=SQUARE)
-            minus_one_times(through[:], tanh_c[:], dh[j][:])
-            return through
+            return tanh_c
 
-        def subtract_incoming(j, minus_dc):
-            incoming = row("incoming")
-            picked(dcn, j, incoming[:])
-            nc.vector.tensor_tensor(out=minus_dc[:], in0=minus_dc[:], in1=incoming[:], op=SUBTRACT)
-
-        def gradients(j, first, count, factors, minus_dc):
+        def gradients(first, count, factors, dc):
             z = work.tile([P, count * WIDTH], BF16, name="z", align_bytes=64)
             nc.vector.tensor_tensor(
                 out=z[:].rearrange("p (g i) -> p g i", g=count),
                 in0=factors[:, first : first + count, :],
-                in1=minus_dc[:].unsqueeze(1).to_broadcast([P, count, WIDTH]),
+                in1=dc[:].unsqueeze(1).to_broadcast([P, count, WIDTH]),
                 op=MULT,
             )
-            grouped = turn(z, count, nc.vector.tensor_copy)
+            return z
+
+        def quantize_gradients(j, first, count, z, copy, tag=None):
+            grouped = turn(z, count, copy, tag)
             for g in range(count):
                 quantize(z_q[first + g], strip(j), grouped[:, g, :], E5M2X4)
 
@@ -145,81 +147,52 @@ def tile_attend_glstm_u_kernel(tc, wo, dy, dcn, gi, gf, go, gc, ct, cp, h0, offs
             grouped = turn(rows, 1, nc.scalar.copy)
             quantize(h0_q, strip(k), grouped[:, 0, :], E4M3X4)
 
-        def ordinary_tile(j):
+        def factors_and_cell(j, squared, z_before):
             gates = work.tile([P, 2, WIDTH], F32, name="gates")
             factors = work.tile([P, 2, WIDTH], F32, name="factors")
+            out_gate = row("out_gate")
+            incoming = row("incoming")
             minus_dc = row("minus_dc")
-            through = through_tanh(j)
-            if j > 0:
-                old_hidden(j)
+            minus_one_times(minus_dc[:], squared[:], dh[j][:])
             picked(gi, j, gates[:, 0, :])
             picked_times(gc, j, gates[:, 0, :], factors[:, 0, :])
-            picked(go, j, minus_dc[:])
-            nc.vector.tensor_tensor(out=minus_dc[:], in0=minus_dc[:], in1=through[:], op=MULT)
-            picked(gf, j, gates[:, 1, :])
+            picked(gf, j, gates[:, 1, :], "gf_%d" % j)
             picked_times(cp, j, gates[:, 1, :], factors[:, 1, :])
+            if z_before is not None:
+                quantize_gradients(j - 1, 0, 2, z_before, nc.scalar.copy, "gf_%d" % j)
             minus_one_times(factors[:], gates[:], factors[:])
-            subtract_incoming(j, minus_dc)
-            gradients(j, 0, 2, factors, minus_dc)
+            picked(go, j, out_gate[:])
+            nc.vector.tensor_tensor(out=minus_dc[:], in0=out_gate[:], in1=minus_dc[:], op=MULT)
+            picked(dcn, j, incoming[:])
+            nc.vector.tensor_tensor(out=minus_dc[:], in0=minus_dc[:], in1=incoming[:], op=SUBTRACT)
+            return factors, minus_dc
 
         def whole_rows(g, k, copy):
             acc = bank()
             product(acc[:], h0_q, strip(k), z_q[g], whole)
-            staged = work.tile([P, WIDTH], F32, name="staged", bufs=TILES + 1)
+            staged = work.tile([P, WIDTH], F32, name="staged", bufs=2 * TILES)
             copy(out=staged[:], in_=acc[:])
             nc.sync.dma_start(out=outs[g][strip(k), :], in_=staged[:])
 
         last = TILES - 1
-        early = last * P
-
-        def early_columns(g):
-            staged = work.tile([P, last, early], F32, name="staged_early", tag="late", bufs=1)
-            for k in range(last):
-                acc = bank()
-                product(acc[:, : 2 * P], h0_q, strip(k), z_q[g], slice(0, 2 * P))
-                product(acc[:, strip(2)], h0_q, strip(k), z_q[g], strip(2))
-                nc.scalar.copy(out=staged[:, k, :], in_=acc[:, :early])
-            nc.sync.dma_start(out=outs[g][:early, :early].rearrange("(k p) h -> p k h", p=P), in_=staged[:])
-
-        def late_columns(g, copy):
-            acc = bank()
-            for k in range(last):
-                product(acc[:, strip(k)], h0_q, strip(k), z_q[g], strip(last))
-            staged = work.tile([P, last, P], F32, name="staged_late", bufs=1)
-            copy(out=staged[:], in_=acc[:, :early].rearrange("p (k h) -> p k h", k=last))
-            nc.sync.dma_start(out=outs[g][:early, strip(last)].rearrange("(k p) h -> p k h", p=P), in_=staged[:])
-
-        def last_tile(j):
-            gates = work.tile([P, 2, WIDTH], F32, name="gates")
-            factors = work.tile([P, 2, WIDTH], F32, name="factors")
-            minus_dc = row("minus_dc")
-            through = through_tanh(j)
-            picked(gi, j, gates[:, 0, :])
-            picked_times(gc, j, gates[:, 0, :], factors[:, 0, :])
-            picked(gf, j, gates[:, 1, :])
-            picked_times(cp, j, gates[:, 1, :], factors[:, 1, :])
-            minus_one_times(factors[:], gates[:], factors[:])
-            picked(go, j, minus_dc[:], "late")
-            nc.vector.tensor_tensor(out=minus_dc[:], in0=minus_dc[:], in1=through[:], op=MULT)
-            subtract_incoming(j, minus_dc)
-            gradients(j, 0, 1, factors, minus_dc)
-            gradients(j, 1, 1, factors, minus_dc)
-            old_hidden(j)
-            early_columns(1)
-            for k in range(last):
-                whole_rows(0, k, nc.scalar.copy)
-            whole_rows(0, last, nc.vector.tensor_copy)
-            whole_rows(1, last, nc.scalar.copy)
-            late_columns(1, nc.vector.tensor_copy)
-
         outs = (out_0, out_1)
         nc.sync.dma_start(out=offsets[:], in_=offs)
-        old_hidden(0)
+        squared = tanh_squared(0)
         quantize_along_m(dy, dy_q, E5M2X4)
         quantize_along_m(wo, wo_q, E4M3X4)
         dh = [bank() for j in range(TILES)]
         for j in range(TILES):
             product(dh[j][:], wo_q, strip(j), dy_q, whole)
+        z = None
         for j in range(last):
-            ordinary_tile(j)
-        last_tile(last)
+            factors, minus_dc = factors_and_cell(j, squared, z)
+            z = gradients(0, 2, factors, minus_dc)
+            squared = tanh_squared(j + 1)
+        factors, minus_dc = factors_and_cell(last, squared, z)
+        for g in range(2):
+            quantize_gradients(last, g, 1, gradients(g, 1, factors, minus_dc), nc.vector.tensor_copy)
+        for k in range(TILES):
+            old_hidden(k)
+        for k in range(TILES):
+            whole_rows(0, k, nc.vector.tensor_copy)
+            whole_rows(1, k, nc.vector.tensor_copy if k < 2 else nc.scalar.copy)

@@ -21,8 +21,8 @@ WIDTH = 512
 SESSIONS = 1024
 TILES = WIDTH // P
 NEIGHBOURS = 4
-WINDOWS = 22
-ACC_BANKS = 6
+WINDOWS = 20
+ACC_BANKS = 5
 TURN_BANKS = 2
 FLOPS = 3 * 2 * WIDTH * WIDTH * WIDTH
 
@@ -92,14 +92,13 @@ def tile_attend_glstm_u_kernel(tc, wo, dy, dcn, gi, gf, go, gc, ct, cp, h0, offs
             )
             quantize(operand, whole, grouped[:], fmt)
 
-        def turn(rows_bf16, count, copy, tag=None):
+        def turn(rows_bf16, count, copy, bank, tag=None):
             words = rows_bf16[:].bitcast(F32).rearrange("p (g w u) -> p g u w", g=count, u=2)
-            bank = psum.tile([P, 2, 2, P], F32, name="turn_bank", bufs=TURN_BANKS)
             for g in range(count):
                 for u in range(2):
                     nc.tensor.transpose(bank[:, g, u, :], words[:, g, u, :], ident[:])
             if tag is None:
-                grouped = work.tile([P, count, WIDTH], BF16, name="grouped_%d" % count, align_bytes=64)
+                grouped = work.tile([P, count, WIDTH], BF16, name="grouped_tail", bufs=2 + TILES, align_bytes=64)
             else:
                 grouped = keep.tile([P, count, WIDTH], BF16, name="grouped", tag=tag, align_bytes=64)
             copy(
@@ -137,14 +136,21 @@ def tile_attend_glstm_u_kernel(tc, wo, dy, dcn, gi, gf, go, gc, ct, cp, h0, offs
             return z
 
         def quantize_gradients(j, first, count, z, copy, tag=None):
-            grouped = turn(z, count, copy, tag)
+            grouped = turn(z, count, copy, psum.tile([P, 2, 2, P], F32, name="z_bank", bufs=TURN_BANKS), tag)
             for g in range(count):
                 quantize(z_q[first + g], strip(j), grouped[:, g, :], E5M2X4)
 
         def old_hidden(k):
-            rows = work.tile([P, WIDTH], BF16, name="old_hidden", align_bytes=64)
-            picked(h0, k, rows[:])
-            grouped = turn(rows, 1, nc.scalar.copy)
+            rows = work.tile([P, WIDTH], BF16, name="old_hidden", bufs=TILES, align_bytes=64)
+            picked(h0, k, rows[:], "h0_%d" % k)
+            return rows
+
+        def quantize_old_hidden(k, rows):
+            if k < last:
+                bank = psum.tile([P, 1, 2, P], F32, name="h0_bank")
+            else:
+                bank = psum.tile([P, 1, 2, P], F32, name="z_bank", bufs=TURN_BANKS)
+            grouped = turn(rows, 1, nc.scalar.copy, bank, "h0_%d" % (k + 1) if k < last else None)
             quantize(h0_q, strip(k), grouped[:, 0, :], E4M3X4)
 
         def factors_and_cell(j, squared, z_before):
@@ -191,8 +197,10 @@ def tile_attend_glstm_u_kernel(tc, wo, dy, dcn, gi, gf, go, gc, ct, cp, h0, offs
         factors, minus_dc = factors_and_cell(last, squared, z)
         for g in range(2):
             quantize_gradients(last, g, 1, gradients(g, 1, factors, minus_dc), nc.vector.tensor_copy)
+        rows = [old_hidden(k) for k in range(TILES)]
+        quantize_old_hidden(0, rows[0])
         for k in range(TILES):
-            old_hidden(k)
-        for k in range(TILES):
-            whole_rows(0, k, nc.vector.tensor_copy)
-            whole_rows(1, k, nc.vector.tensor_copy if k < 2 else nc.scalar.copy)
+            if k < last:
+                quantize_old_hidden(k + 1, rows[k + 1])
+            whole_rows(0, k, nc.scalar.copy if k == 2 else nc.vector.tensor_copy)
+            whole_rows(1, k, nc.scalar.copy if k >= 2 else nc.vector.tensor_copy)

@@ -125,6 +125,18 @@ def tile_attend_glstm_u_kernel(tc, wo, dy, dcn, gi, gf, go, gc, ct, cp, h0, offs
             nc.scalar.activation(out=tanh_c[:], in_=tanh_c[:], func=SQUARE)
             return tanh_c
 
+        def gradients_from_dc(factors, dc):
+            z = work.tile([P, 2 * WIDTH], BF16, name="z", align_bytes=64)
+            nc.vector.scalar_tensor_tensor(
+                out=z[:].rearrange("p (g i) -> p g i", g=2),
+                in0=factors[:],
+                scalar=-1.0,
+                in1=dc[:].unsqueeze(1).to_broadcast([P, 2, WIDTH]),
+                op0=MULT,
+                op1=MULT,
+            )
+            return z
+
         def gradients(first, count, factors, dc):
             z = work.tile([P, count * WIDTH], BF16, name="z", align_bytes=64)
             nc.vector.tensor_tensor(
@@ -169,6 +181,9 @@ def tile_attend_glstm_u_kernel(tc, wo, dy, dcn, gi, gf, go, gc, ct, cp, h0, offs
             minus_one_times(factors[:], gates[:], factors[:])
             picked(go, j, out_gate[:])
             nc.vector.tensor_tensor(out=minus_dc[:], in0=out_gate[:], in1=minus_dc[:], op=MULT)
+            if j < last:
+                nc.vector.tensor_tensor(out=incoming[:], in0=listed(load_rows(dcn, j)), in1=minus_dc[:], op=SUBTRACT)
+                return factors, incoming
             picked(dcn, j, incoming[:])
             nc.vector.tensor_tensor(out=minus_dc[:], in0=minus_dc[:], in1=incoming[:], op=SUBTRACT)
             return factors, minus_dc
@@ -192,7 +207,7 @@ def tile_attend_glstm_u_kernel(tc, wo, dy, dcn, gi, gf, go, gc, ct, cp, h0, offs
         z = None
         for j in range(last):
             factors, minus_dc = factors_and_cell(j, squared, z)
-            z = gradients(0, 2, factors, minus_dc)
+            z = gradients_from_dc(factors, minus_dc)
             squared = tanh_squared(j + 1)
         factors, minus_dc = factors_and_cell(last, squared, z)
         for g in range(2):

@@ -162,7 +162,10 @@ def tile_attend_glstm_u_kernel(tc, wo, dy, dcn, gi, gf, go, gc, ct, cp, h0, offs
                 bank = psum.tile([P, 1, 2, P], F32, name="h0_bank")
             else:
                 bank = psum.tile([P, 1, 2, P], F32, name="z_bank", bufs=TURN_BANKS)
-            grouped = turn(rows, 1, nc.scalar.copy, bank, "h0_%d" % (k + 1) if k < last else None)
+            if k == 0:
+                grouped = turn(rows, 1, nc.vector.tensor_copy, bank)
+            else:
+                grouped = turn(rows, 1, nc.scalar.copy, bank, "h0_%d" % (k + 1) if k < last else None)
             quantize(h0_q, strip(k), grouped[:, 0, :], E4M3X4)
 
         def factors_and_cell(j, squared, z_before):
@@ -210,10 +213,11 @@ def tile_attend_glstm_u_kernel(tc, wo, dy, dcn, gi, gf, go, gc, ct, cp, h0, offs
             z = gradients_from_dc(factors, minus_dc)
             squared = tanh_squared(j + 1)
         factors, minus_dc = factors_and_cell(last, squared, z)
-        for g in range(2):
-            quantize_gradients(last, g, 1, gradients(g, 1, factors, minus_dc), nc.vector.tensor_copy)
+        z = [gradients(g, 1, factors, minus_dc) for g in range(2)]
         rows = [old_hidden(k) for k in range(TILES)]
         quantize_old_hidden(0, rows[0])
+        quantize_gradients(last, 0, 1, z[0], nc.vector.tensor_copy)
+        quantize_gradients(last, 1, 1, z[1], nc.vector.tensor_copy)
         for k in range(TILES):
             if k < last:
                 quantize_old_hidden(k + 1, rows[k + 1])

@@ -92,8 +92,9 @@ def tile_attend_glstm_u_kernel(tc, wo, dy, dcn, gi, gf, go, gc, ct, cp, h0, offs
             )
             quantize(operand, whole, grouped[:], fmt)
 
-        def turn(rows_bf16, count, copy, bank, tag=None):
-            words = rows_bf16[:].bitcast(F32).rearrange("p (g w u) -> p g u w", g=count, u=2)
+        def turn(rows_bf16, count, copy, bank, tag=None, sorted_words=False):
+            order = "p (g u w) -> p g u w" if sorted_words else "p (g w u) -> p g u w"
+            words = rows_bf16[:].bitcast(F32).rearrange(order, g=count, u=2)
             for g in range(count):
                 for u in range(2):
                     nc.tensor.transpose(bank[:, g, u, :], words[:, g, u, :], ident[:])
@@ -140,15 +141,15 @@ def tile_attend_glstm_u_kernel(tc, wo, dy, dcn, gi, gf, go, gc, ct, cp, h0, offs
         def gradients(first, count, factors, dc):
             z = work.tile([P, count * WIDTH], BF16, name="z", align_bytes=64)
             nc.vector.tensor_tensor(
-                out=z[:].rearrange("p (g i) -> p g i", g=count),
-                in0=factors[:, first : first + count, :],
-                in1=dc[:].unsqueeze(1).to_broadcast([P, count, WIDTH]),
+                out=z[:].rearrange("p (u w e) -> p u w e", u=2, e=2),
+                in0=factors[:, first, :].rearrange("p (w u e) -> p u w e", u=2, e=2),
+                in1=dc[:].rearrange("p (w u e) -> p u w e", u=2, e=2),
                 op=MULT,
             )
             return z
 
         def quantize_gradients(j, first, count, z, copy, tag=None):
-            grouped = turn(z, count, copy, psum.tile([P, 2, 2, P], F32, name="z_bank", bufs=TURN_BANKS), tag)
+            grouped = turn(z, count, copy, psum.tile([P, 2, 2, P], F32, name="z_bank", bufs=TURN_BANKS), tag, count == 1)
             for g in range(count):
                 quantize(z_q[first + g], strip(j), grouped[:, g, :], E5M2X4)
 

@@ -20,10 +20,11 @@ PACK = 4
 WIDTH = 512
 SESSIONS = 1024
 TILES = WIDTH // P
+GATES = 2
 NEIGHBOURS = 4
-WINDOWS = 20
-ACC_BANKS = 5
 TURN_BANKS = 2
+WINDOW_BYTES = 4 * SESSIONS
+HELD_BYTES = 4 * WIDTH
 FLOPS = 3 * 2 * WIDTH * WIDTH * WIDTH
 
 
@@ -31,38 +32,49 @@ def tile_attend_glstm_u_kernel(tc, wo, dy, dcn, gi, gf, go, gc, ct, cp, h0, offs
     nc = tc.nc
     with ExitStack() as ctx:
         keep = ctx.enter_context(tc.tile_pool(name="keep", bufs=1))
+        placed = ctx.enter_context(tc.tile_pool(name="placed", bufs=1))
         work = ctx.enter_context(tc.tile_pool(name="work", bufs=2))
         psum = ctx.enter_context(tc.psum_pool(name="psum", bufs=1))
+
+        last = TILES - 1
+        outs = (out_0, out_1)
+        tables = {"h0": h0, "ct": ct, "gi": gi, "gc": gc, "gf": gf, "cp": cp, "go": go, "dcn": dcn}
+        stage_order = ("ct", "gi", "go", "gf", "gc", "dcn", "cp")
+        last_order = ("ct", "gi", "go", "gf", "dcn", "gc", "cp")
 
         offsets = keep.tile([P, WIDTH // 16], U16, name="offsets")
         ident = keep.tile([P, P], F32, name="ident")
         make_identity(nc, ident[:])
 
-        def quantized(name, columns):
-            codes = keep.tile([P, columns], U32, name=name + "_codes", align_bytes=64)
-            scales = keep.tile([P, columns], U8, name=name + "_scales", align_bytes=64)
-            return codes, scales
-
-        wo_q = quantized("wo", WIDTH)
-        dy_q = quantized("dy", WIDTH)
-        h0_q = quantized("h0", WIDTH)
-        z_q = [quantized("zi", WIDTH), quantized("zf", WIDTH)]
-
         def strip(j):
             return slice(j * P, (j + 1) * P)
 
         whole = slice(0, WIDTH)
+        windows = {}
+        places = {}
 
-        def load_rows(table, j, tag=None):
-            if tag is None:
-                window = work.tile([P, SESSIONS], F32, name="window", bufs=WINDOWS)
-            else:
-                window = keep.tile([P, SESSIONS], F32, name="window", tag=tag, align_bytes=64)
-            nc.sync.dma_start(out=window[:], in_=table[strip(j), :])
-            return window
+        def load_rows(name, j):
+            place = len(windows) * WINDOW_BYTES + (HELD_BYTES if (name, j) == ("gf", 2) else 0) + (WINDOW_BYTES if ("gf", 2) in windows else 0)
+            window = placed.tile([P, SESSIONS], F32, name="%s_%d" % (name, j), offset=place, align_bytes=64)
+            nc.sync.dma_start(out=window[:], in_=tables[name][strip(j), :])
+            windows[name, j] = window
+            places[name, j] = place
 
-        def listed(window):
-            return window[:].indirect(offsets[:])
+        def load_along_m(src, name):
+            raw = keep.tile([P, PACK, WIDTH], F32, name=name)
+            nc.sync.dma_start(out=raw[:], in_=src.rearrange("(p t) c -> p t c", t=PACK))
+            return raw
+
+        def held(shape, dtype, name, behind, shift):
+            return placed.tile(shape, dtype, name=name, offset=places[behind] + shift, align_bytes=64)
+
+        def listed(name, j):
+            return windows[name, j][:].indirect(offsets[:])
+
+        def quantized(name, columns):
+            codes = keep.tile([P, columns], U32, name=name + "_codes", align_bytes=64)
+            scales = keep.tile([P, columns], U8, name=name + "_scales", align_bytes=64)
+            return codes, scales
 
         def quantize(operand, cols, grouped, fmt):
             codes, scales = operand
@@ -79,12 +91,10 @@ def tile_attend_glstm_u_kernel(tc, wo, dy, dcn, gi, gf, go, gc, ct, cp, h0, offs
                 stop=True,
             )
 
-        def bank():
-            return psum.tile([P, WIDTH], F32, name="acc", bufs=ACC_BANKS)
+        def bank(tag):
+            return psum.tile([P, WIDTH], F32, name="acc", tag=tag)
 
-        def quantize_along_m(src, operand, fmt):
-            raw = work.tile([P, PACK, WIDTH], F32, name="raw")
-            nc.sync.dma_start(out=raw[:], in_=src.rearrange("(p t) c -> p t c", t=PACK))
+        def quantize_along_m(raw, operand, fmt):
             grouped = work.tile([P, WIDTH * PACK], BF16, name="grouped_m", align_bytes=64)
             nc.vector.tensor_copy(
                 out=grouped[:].rearrange("p (c i t) -> p c t i", i=NEIGHBOURS, t=PACK),
@@ -92,27 +102,23 @@ def tile_attend_glstm_u_kernel(tc, wo, dy, dcn, gi, gf, go, gc, ct, cp, h0, offs
             )
             quantize(operand, whole, grouped[:], fmt)
 
-        def turn(rows_bf16, count, copy, bank, tag=None, sorted_words=False):
+        def turn(rows_bf16, count, copy, grouped, sorted_words=False):
+            turned = psum.tile([P, GATES, 2, P], F32, name="turned", bufs=TURN_BANKS)
             order = "p (g u w) -> p g u w" if sorted_words else "p (g w u) -> p g u w"
             words = rows_bf16[:].bitcast(F32).rearrange(order, g=count, u=2)
             for g in range(count):
                 for u in range(2):
-                    nc.tensor.transpose(bank[:, g, u, :], words[:, g, u, :], ident[:])
-            if tag is None:
-                grouped = work.tile([P, count, WIDTH], BF16, name="grouped_tail", bufs=2 + TILES, align_bytes=64)
-            else:
-                grouped = keep.tile([P, count, WIDTH], BF16, name="grouped", tag=tag, align_bytes=64)
+                    nc.tensor.transpose(turned[:, g, u, :], words[:, g, u, :], ident[:])
             copy(
-                out=grouped[:].bitcast(F32).rearrange("p g (c u) -> p g c u", u=2),
-                in_=bank[:, :count, :, :].rearrange("p g u c -> p g c u"),
+                out=grouped[:].bitcast(F32).rearrange("p (g c u) -> p g c u", g=count, u=2),
+                in_=turned[:, :count, :, :].rearrange("p g u c -> p g c u"),
             )
-            return grouped
 
-        def picked(table, j, out, tag=None):
-            nc.scalar.activation(out=out, in_=listed(load_rows(table, j, tag)), func=COPY)
+        def picked(name, j, out):
+            nc.scalar.activation(out=out, in_=listed(name, j), func=COPY)
 
-        def picked_times(table, j, other, out):
-            nc.vector.tensor_tensor(out=out, in0=listed(load_rows(table, j)), in1=other, op=MULT)
+        def picked_with(name, j, other, op, out):
+            nc.vector.tensor_tensor(out=out, in0=listed(name, j), in1=other, op=op)
 
         def row(name):
             return work.tile([P, WIDTH], F32, name=name)
@@ -120,107 +126,135 @@ def tile_attend_glstm_u_kernel(tc, wo, dy, dcn, gi, gf, go, gc, ct, cp, h0, offs
         def minus_one_times(out, in0, in1):
             nc.vector.scalar_tensor_tensor(out=out, in0=in0, scalar=1.0, in1=in1, op0=SUBTRACT, op1=MULT)
 
-        def tanh_squared(j):
-            tanh_c = row("tanh_c")
-            picked(ct, j, tanh_c[:])
-            nc.scalar.activation(out=tanh_c[:], in_=tanh_c[:], func=SQUARE)
-            return tanh_c
+        def negated_product(out, in0, in1):
+            nc.vector.scalar_tensor_tensor(out=out, in0=in0, scalar=-1.0, in1=in1, op0=MULT, op1=MULT)
 
-        def gradients_from_dc(factors, dc):
-            z = work.tile([P, 2 * WIDTH], BF16, name="z", align_bytes=64)
-            nc.vector.scalar_tensor_tensor(
-                out=z[:].rearrange("p (g i) -> p g i", g=2),
-                in0=factors[:],
-                scalar=-1.0,
-                in1=dc[:].unsqueeze(1).to_broadcast([P, 2, WIDTH]),
-                op0=MULT,
-                op1=MULT,
-            )
-            return z
-
-        def gradients(first, count, factors, dc):
-            z = work.tile([P, count * WIDTH], BF16, name="z", align_bytes=64)
-            nc.vector.tensor_tensor(
-                out=z[:].rearrange("p (u w e) -> p u w e", u=2, e=2),
-                in0=factors[:, first, :].rearrange("p (w u e) -> p u w e", u=2, e=2),
-                in1=dc[:].rearrange("p (w u e) -> p u w e", u=2, e=2),
-                op=MULT,
-            )
-            return z
-
-        def quantize_gradients(j, first, count, z, copy, tag=None):
-            grouped = turn(z, count, copy, psum.tile([P, 2, 2, P], F32, name="z_bank", bufs=TURN_BANKS), tag, count == 1)
-            for g in range(count):
-                quantize(z_q[first + g], strip(j), grouped[:, g, :], E5M2X4)
-
-        def old_hidden(k):
+        def quantize_old_hidden(k):
             rows = work.tile([P, WIDTH], BF16, name="old_hidden", bufs=TILES, align_bytes=64)
-            picked(h0, k, rows[:], "h0_%d" % k)
-            return rows
+            picked("h0", k, rows[:])
+            grouped = work.tile([P, WIDTH], BF16, name="grouped_row", bufs=TILES, align_bytes=64)
+            turn(rows, 1, nc.vector.tensor_copy, grouped)
+            quantize(h0_q, strip(k), grouped[:], E4M3X4)
 
-        def quantize_old_hidden(k, rows):
-            if k < last:
-                bank = psum.tile([P, 1, 2, P], F32, name="h0_bank")
-            else:
-                bank = psum.tile([P, 1, 2, P], F32, name="z_bank", bufs=TURN_BANKS)
-            if k == 0:
-                grouped = turn(rows, 1, nc.vector.tensor_copy, bank)
-            else:
-                grouped = turn(rows, 1, nc.scalar.copy, bank, "h0_%d" % (k + 1) if k < last else None)
-            quantize(h0_q, strip(k), grouped[:, 0, :], E4M3X4)
+        def through_tanh(j):
+            tanh_c = row("tanh_c")
+            picked("ct", j, tanh_c[:])
+            nc.scalar.activation(out=tanh_c[:], in_=tanh_c[:], func=SQUARE)
+            minus_back = row("minus_back")
+            minus_one_times(minus_back[:], tanh_c[:], dh[j][:])
+            return minus_back
 
-        def factors_and_cell(j, squared, z_before):
-            gates = work.tile([P, 2, WIDTH], F32, name="gates")
-            factors = work.tile([P, 2, WIDTH], F32, name="factors")
-            out_gate = row("out_gate")
-            incoming = row("incoming")
-            minus_dc = row("minus_dc")
-            minus_one_times(minus_dc[:], squared[:], dh[j][:])
-            picked(gi, j, gates[:, 0, :])
-            picked_times(gc, j, gates[:, 0, :], factors[:, 0, :])
-            picked(gf, j, gates[:, 1, :], "gf_%d" % j)
-            picked_times(cp, j, gates[:, 1, :], factors[:, 1, :])
-            if z_before is not None:
-                quantize_gradients(j - 1, 0, 2, z_before, nc.scalar.copy, "gf_%d" % j)
-            minus_one_times(factors[:], gates[:], factors[:])
-            picked(go, j, out_gate[:])
-            nc.vector.tensor_tensor(out=minus_dc[:], in0=out_gate[:], in1=minus_dc[:], op=MULT)
-            if j < last:
-                nc.vector.tensor_tensor(out=incoming[:], in0=listed(load_rows(dcn, j)), in1=minus_dc[:], op=SUBTRACT)
-                return factors, incoming
-            picked(dcn, j, incoming[:])
-            nc.vector.tensor_tensor(out=minus_dc[:], in0=minus_dc[:], in1=incoming[:], op=SUBTRACT)
-            return factors, minus_dc
+        def output_strip(j, g, tag):
+            acc = bank(tag)
+            for k in range(TILES):
+                product(acc[:, strip(k)], h0_q, strip(k), z_q[j], strip(g))
+            return acc[:].rearrange("p (k c) -> p k c", k=TILES)
 
-        def whole_rows(g, k, copy):
-            acc = bank()
-            product(acc[:], h0_q, strip(k), z_q[g], whole)
-            staged = work.tile([P, WIDTH], F32, name="staged", bufs=2 * TILES)
-            copy(out=staged[:], in_=acc[:])
-            nc.sync.dma_start(out=outs[g][strip(k), :], in_=staged[:])
+        def quantize_gradients(j, z, grouped):
+            turn(z, GATES, nc.scalar.copy, grouped)
+            quantize(z_q[j], slice(0, GATES * P), grouped[:], E5M2X4)
 
-        last = TILES - 1
-        outs = (out_0, out_1)
+        def store(g, cols, staged):
+            nc.sync.dma_start(out=outs[g][:, cols].rearrange("(k p) c -> p k c", p=P), in_=staged[:])
+
+        load_rows("h0", 0)
         nc.sync.dma_start(out=offsets[:], in_=offs)
-        squared = tanh_squared(0)
-        quantize_along_m(dy, dy_q, E5M2X4)
-        quantize_along_m(wo, wo_q, E4M3X4)
-        dh = [bank() for j in range(TILES)]
+        dy_raw = load_along_m(dy, "dy_raw")
+        wo_raw = load_along_m(wo, "wo_raw")
+        for k in range(1, TILES):
+            load_rows("h0", k)
+        for j in range(TILES):
+            for name in stage_order if j < last else last_order:
+                load_rows(name, j)
+
+        wo_q = quantized("wo", WIDTH)
+        dy_q = quantized("dy", WIDTH)
+        h0_q = quantized("h0", WIDTH)
+        z_q = [quantized("z%d" % j, GATES * P) for j in range(TILES)]
+
+        quantize_old_hidden(0)
+        quantize_along_m(dy_raw, dy_q, E5M2X4)
+        quantize_along_m(wo_raw, wo_q, E4M3X4)
+        dh = [bank("dh%d" % j) for j in range(TILES)]
         for j in range(TILES):
             product(dh[j][:], wo_q, strip(j), dy_q, whole)
+        for k in range(1, TILES):
+            quantize_old_hidden(k)
+
+        def slope(name, j):
+            gate = row("gate")
+            picked(name, j, gate[:])
+            minus_slope = row("minus_slope_" + name)
+            minus_one_times(minus_slope[:], gate[:], gate[:])
+            return minus_slope
+
+        def front(j):
+            minus_back = through_tanh(j)
+            slope_i = slope("gi", j)
+            gated = row("gated")
+            picked_with("go", j, minus_back[:], MULT, gated[:])
+            return gated, [slope_i, slope("gf", j)]
+
+        def turned_behind_gi(j, z):
+            grouped = held([P, GATES * WIDTH], BF16, "grouped_z%d" % (j - 1), ("gi", j), 0)
+            quantize_gradients(j - 1, z, grouped)
+
+        pairs = []
         z = None
         for j in range(last):
-            factors, minus_dc = factors_and_cell(j, squared, z)
-            z = gradients_from_dc(factors, minus_dc)
-            squared = tanh_squared(j + 1)
-        factors, minus_dc = factors_and_cell(last, squared, z)
-        z = [gradients(g, 1, factors, minus_dc) for g in range(2)]
-        rows = [old_hidden(k) for k in range(TILES)]
-        quantize_old_hidden(0, rows[0])
-        quantize_gradients(last, 0, 1, z[0], nc.vector.tensor_copy)
-        quantize_gradients(last, 1, 1, z[1], nc.vector.tensor_copy)
-        for k in range(TILES):
-            if k < last:
-                quantize_old_hidden(k + 1, rows[k + 1])
-            whole_rows(0, k, nc.scalar.copy if k == 2 else nc.vector.tensor_copy)
-            whole_rows(1, k, nc.scalar.copy if k >= 2 else nc.vector.tensor_copy)
+            gated, slopes = front(j)
+            if j >= 1:
+                turned_behind_gi(j, z)
+            if j == 2:
+                for g in range(GATES):
+                    shift = g * WINDOW_BYTES - HELD_BYTES
+                    pairs.append(held([P, TILES, 2 * P], F32, "staged_pair%d" % g, ("gf", j), shift))
+                    nc.scalar.copy(out=pairs[g][:, :, strip(0)], in_=output_strip(0, g, "out%d" % g))
+                for g in range(GATES):
+                    nc.scalar.copy(out=pairs[g][:, :, strip(1)], in_=output_strip(1, g, "dh%d" % g))
+                    store(g, slice(0, 2 * P), pairs[g])
+            minus_factor = row("minus_factor")
+            picked_with("gc", j, slopes[0][:], MULT, minus_factor[:])
+            dc = row("dc")
+            picked_with("dcn", j, gated[:], SUBTRACT, dc[:])
+            negated_product(slopes[1][:], slopes[1][:], dc[:])
+            z = work.tile([P, GATES * WIDTH], BF16, name="z", align_bytes=64)
+            negated_product(z[:, :WIDTH], minus_factor[:], dc[:])
+            old_cell = row("partner")
+            picked("cp", j, old_cell[:])
+            nc.vector.tensor_tensor(out=z[:, WIDTH:], in0=old_cell[:], in1=slopes[1][:], op=MULT)
+
+        gated, slopes = front(last)
+        turned_behind_gi(last, z)
+        dc = row("dc")
+        picked_with("dcn", last, gated[:], SUBTRACT, dc[:])
+        accs = [output_strip(last - 1, g, "out%d" % g) for g in range(GATES)]
+        for g in range(GATES):
+            negated_product(slopes[g][:], slopes[g][:], dc[:])
+        rows = []
+        for g, name in ((0, "gc"), (1, "cp")):
+            partner = row("partner")
+            picked(name, last, partner[:])
+            z = work.tile([P, WIDTH], BF16, name="z_last", align_bytes=64)
+            nc.vector.tensor_tensor(
+                out=z[:].rearrange("p (u w e) -> p u w e", u=2, e=2),
+                in0=partner[:].rearrange("p (w u e) -> p u w e", u=2, e=2),
+                in1=slopes[g][:].rearrange("p (w u e) -> p u w e", u=2, e=2),
+                op=MULT,
+            )
+            rows.append(z)
+        for g in range(GATES):
+            staged = held([P, TILES, P], F32, "staged_strip%d" % g, ("cp", last), g * (HELD_BYTES + HELD_BYTES // 2))
+            nc.scalar.copy(out=staged[:], in_=accs[g])
+            store(g, strip(last - 1), staged)
+            if g == 0:
+                grouped = held([P, WIDTH], BF16, "grouped_zi", ("cp", last), HELD_BYTES)
+                turn(rows[g], 1, nc.scalar.copy, grouped, True)
+                quantize(z_q[last], strip(g), grouped[:], E5M2X4)
+        grouped = work.tile([P, WIDTH], BF16, name="grouped_row", bufs=TILES, align_bytes=64)
+        turn(rows[1], 1, nc.vector.tensor_copy, grouped, True)
+        quantize(z_q[last], strip(1), grouped[:], E5M2X4)
+        for g, copy in ((0, nc.scalar.copy), (1, nc.vector.tensor_copy)):
+            staged = work.tile([P, TILES, P], F32, name="staged_last")
+            copy(out=staged[:], in_=output_strip(last, g, "dh%d" % g))
+            store(g, strip(last), staged)

@@ -39,8 +39,7 @@ def tile_attend_glstm_u_kernel(tc, wo, dy, dcn, gi, gf, go, gc, ct, cp, h0, offs
         last = TILES - 1
         outs = (out_0, out_1)
         tables = {"h0": h0, "ct": ct, "gi": gi, "gc": gc, "gf": gf, "cp": cp, "go": go, "dcn": dcn}
-        stage_order = ("ct", "gi", "go", "gf", "gc", "dcn", "cp")
-        last_order = ("ct", "gi", "go", "gf", "dcn", "gc", "cp")
+        stage_order = ("ct", "go", "gi", "gf", "gc", "dcn", "cp")
 
         offsets = keep.tile([P, WIDTH // 16], U16, name="offsets")
         ident = keep.tile([P, P], F32, name="ident")
@@ -54,7 +53,7 @@ def tile_attend_glstm_u_kernel(tc, wo, dy, dcn, gi, gf, go, gc, ct, cp, h0, offs
         places = {}
 
         def load_rows(name, j):
-            place = len(windows) * WINDOW_BYTES + (HELD_BYTES if (name, j) == ("gf", 2) else 0) + (WINDOW_BYTES if ("gf", 2) in windows else 0)
+            place = len(windows) * WINDOW_BYTES + (WINDOW_BYTES if (name, j) == ("gf", 2) else 0) + (2 * WINDOW_BYTES if ("gf", 2) in windows else 0)
             window = placed.tile([P, SESSIONS], F32, name="%s_%d" % (name, j), offset=place, align_bytes=64)
             nc.sync.dma_start(out=window[:], in_=tables[name][strip(j), :])
             windows[name, j] = window
@@ -71,8 +70,11 @@ def tile_attend_glstm_u_kernel(tc, wo, dy, dcn, gi, gf, go, gc, ct, cp, h0, offs
         def listed(name, j):
             return windows[name, j][:].indirect(offsets[:])
 
-        def quantized(name, columns):
-            codes = keep.tile([P, columns], U32, name=name + "_codes", align_bytes=64)
+        def quantized(name, columns, behind=None):
+            if behind is None:
+                codes = keep.tile([P, columns], U32, name=name + "_codes", align_bytes=64)
+            else:
+                codes = held([P, columns], U32, name + "_codes", behind, 0)
             scales = keep.tile([P, columns], U8, name=name + "_scales", align_bytes=64)
             return codes, scales
 
@@ -102,9 +104,9 @@ def tile_attend_glstm_u_kernel(tc, wo, dy, dcn, gi, gf, go, gc, ct, cp, h0, offs
             )
             quantize(operand, whole, grouped[:], fmt)
 
-        def turn(rows_bf16, count, copy, grouped, sorted_words=False):
+        def turn(rows_bf16, count, copy, grouped, is_sorted=False):
             turned = psum.tile([P, GATES, 2, P], F32, name="turned", bufs=TURN_BANKS)
-            order = "p (g u w) -> p g u w" if sorted_words else "p (g w u) -> p g u w"
+            order = "p (g u w) -> p g u w" if is_sorted else "p (g w u) -> p g u w"
             words = rows_bf16[:].bitcast(F32).rearrange(order, g=count, u=2)
             for g in range(count):
                 for u in range(2):
@@ -150,8 +152,8 @@ def tile_attend_glstm_u_kernel(tc, wo, dy, dcn, gi, gf, go, gc, ct, cp, h0, offs
                 product(acc[:, strip(k)], h0_q, strip(k), z_q[j], strip(g))
             return acc[:].rearrange("p (k c) -> p k c", k=TILES)
 
-        def quantize_gradients(j, z, grouped):
-            turn(z, GATES, nc.scalar.copy, grouped)
+        def quantize_gradients(j, grouped, behind=None):
+            z_q.append(quantized("z%d" % j, GATES * P, behind))
             quantize(z_q[j], slice(0, GATES * P), grouped[:], E5M2X4)
 
         def store(g, cols, staged):
@@ -164,13 +166,13 @@ def tile_attend_glstm_u_kernel(tc, wo, dy, dcn, gi, gf, go, gc, ct, cp, h0, offs
         for k in range(1, TILES):
             load_rows("h0", k)
         for j in range(TILES):
-            for name in stage_order if j < last else last_order:
+            for name in stage_order:
                 load_rows(name, j)
 
         wo_q = quantized("wo", WIDTH)
         dy_q = quantized("dy", WIDTH)
         h0_q = quantized("h0", WIDTH)
-        z_q = [quantized("z%d" % j, GATES * P) for j in range(TILES)]
+        z_q = []
 
         quantize_old_hidden(0)
         quantize_along_m(dy_raw, dy_q, E5M2X4)
@@ -188,68 +190,62 @@ def tile_attend_glstm_u_kernel(tc, wo, dy, dcn, gi, gf, go, gc, ct, cp, h0, offs
             minus_one_times(minus_slope[:], gate[:], gate[:])
             return minus_slope
 
-        def front(j):
-            minus_back = through_tanh(j)
-            slope_i = slope("gi", j)
-            gated = row("gated")
-            picked_with("go", j, minus_back[:], MULT, gated[:])
-            return gated, [slope_i, slope("gf", j)]
+        def sorted_words(rows):
+            return rows.rearrange("p (u w e) -> p u w e", u=2, e=2)
 
-        def turned_behind_gi(j, z):
-            grouped = held([P, GATES * WIDTH], BF16, "grouped_z%d" % (j - 1), ("gi", j), 0)
-            quantize_gradients(j - 1, z, grouped)
+        def words_by_parity(rows):
+            return rows.rearrange("p (w u e) -> p u w e", u=2, e=2)
 
         pairs = []
+        turned_z = []
         z = None
-        for j in range(last):
-            gated, slopes = front(j)
+        for j in range(TILES):
+            minus_back = through_tanh(j)
+            gated = row("gated")
+            picked_with("go", j, minus_back[:], MULT, gated[:])
+            slope_i = slope("gi", j)
+            if j >= 2:
+                quantize_gradients(j - 2, turned_z[j - 2], ("gi", j))
+            slope_f = slope("gf", j)
             if j >= 1:
-                turned_behind_gi(j, z)
-            if j == 2:
-                for g in range(GATES):
-                    shift = g * WINDOW_BYTES - HELD_BYTES
+                turned_z.append(held([P, GATES * WIDTH], BF16, "grouped_z%d" % (j - 1), ("gf", j), HELD_BYTES // 2))
+                turn(z, GATES, nc.scalar.copy, turned_z[j - 1])
+            for g in range(GATES if j >= 2 else 0):
+                if j == 2:
+                    shift = HELD_BYTES // 2 - WINDOW_BYTES if g == 0 else HELD_BYTES + HELD_BYTES // 2
                     pairs.append(held([P, TILES, 2 * P], F32, "staged_pair%d" % g, ("gf", j), shift))
-                    nc.scalar.copy(out=pairs[g][:, :, strip(0)], in_=output_strip(0, g, "out%d" % g))
-                for g in range(GATES):
-                    nc.scalar.copy(out=pairs[g][:, :, strip(1)], in_=output_strip(1, g, "dh%d" % g))
+                nc.scalar.copy(out=pairs[g][:, :, strip(j - 2)], in_=output_strip(j - 2, g, "out%d" % g))
+                if j == last:
                     store(g, slice(0, 2 * P), pairs[g])
             minus_factor = row("minus_factor")
-            picked_with("gc", j, slopes[0][:], MULT, minus_factor[:])
+            picked_with("gc", j, slope_i[:], MULT, minus_factor[:])
             dc = row("dc")
             picked_with("dcn", j, gated[:], SUBTRACT, dc[:])
-            negated_product(slopes[1][:], slopes[1][:], dc[:])
-            z = work.tile([P, GATES * WIDTH], BF16, name="z", align_bytes=64)
-            negated_product(z[:, :WIDTH], minus_factor[:], dc[:])
-            old_cell = row("partner")
-            picked("cp", j, old_cell[:])
-            nc.vector.tensor_tensor(out=z[:, WIDTH:], in0=old_cell[:], in1=slopes[1][:], op=MULT)
+            if j == last:
+                quantize_gradients(j - 1, turned_z[j - 1])
+                accs = [output_strip(j - 1, g, "dh%d" % (g + GATES)) for g in range(GATES)]
+            negated_product(slope_f[:], slope_f[:], dc[:])
+            old_cell = row("old_cell")
+            if j < last:
+                z = work.tile([P, GATES * WIDTH], BF16, name="z", align_bytes=64)
+                negated_product(z[:, :WIDTH], minus_factor[:], dc[:])
+                picked("cp", j, old_cell[:])
+                nc.vector.tensor_tensor(out=z[:, WIDTH:], in0=old_cell[:], in1=slope_f[:], op=MULT)
 
-        gated, slopes = front(last)
-        turned_behind_gi(last, z)
-        dc = row("dc")
-        picked_with("dcn", last, gated[:], SUBTRACT, dc[:])
-        accs = [output_strip(last - 1, g, "out%d" % g) for g in range(GATES)]
-        for g in range(GATES):
-            negated_product(slopes[g][:], slopes[g][:], dc[:])
-        rows = []
-        for g, name in ((0, "gc"), (1, "cp")):
-            partner = row("partner")
-            picked(name, last, partner[:])
-            z = work.tile([P, WIDTH], BF16, name="z_last", align_bytes=64)
-            nc.vector.tensor_tensor(
-                out=z[:].rearrange("p (u w e) -> p u w e", u=2, e=2),
-                in0=partner[:].rearrange("p (w u e) -> p u w e", u=2, e=2),
-                in1=slopes[g][:].rearrange("p (w u e) -> p u w e", u=2, e=2),
-                op=MULT,
-            )
-            rows.append(z)
+        rows = [work.tile([P, WIDTH], BF16, name="z_last", align_bytes=64) for g in range(GATES)]
+        negated_product(rows[0][:], minus_factor[:], dc[:])
+        picked("cp", last, old_cell[:])
+        nc.vector.tensor_tensor(
+            out=sorted_words(rows[1][:]), in0=words_by_parity(old_cell[:]), in1=words_by_parity(slope_f[:]), op=MULT
+        )
+        z_q.append(quantized("z%d" % last, GATES * P))
         for g in range(GATES):
             staged = held([P, TILES, P], F32, "staged_strip%d" % g, ("cp", last), g * (HELD_BYTES + HELD_BYTES // 2))
             nc.scalar.copy(out=staged[:], in_=accs[g])
             store(g, strip(last - 1), staged)
             if g == 0:
                 grouped = held([P, WIDTH], BF16, "grouped_zi", ("cp", last), HELD_BYTES)
-                turn(rows[g], 1, nc.scalar.copy, grouped, True)
+                turn(rows[g], 1, nc.scalar.copy, grouped)
                 quantize(z_q[last], strip(g), grouped[:], E5M2X4)
         grouped = work.tile([P, WIDTH], BF16, name="grouped_row", bufs=TILES, align_bytes=64)
         turn(rows[1], 1, nc.vector.tensor_copy, grouped, True)

@@ -23,6 +23,8 @@ TILES = WIDTH // P
 GATES = 2
 NEIGHBOURS = 4
 TURN_BANKS = 2
+ACC_BANKS = 5
+WINDOWS = 21
 WINDOW_BYTES = 4 * SESSIONS
 HELD_BYTES = 4 * WIDTH
 FLOPS = 3 * 2 * WIDTH * WIDTH * WIDTH
@@ -39,7 +41,8 @@ def tile_attend_glstm_u_kernel(tc, wo, dy, dcn, gi, gf, go, gc, ct, cp, h0, offs
         last = TILES - 1
         outs = (out_0, out_1)
         tables = {"h0": h0, "ct": ct, "gi": gi, "gc": gc, "gf": gf, "cp": cp, "go": go, "dcn": dcn}
-        stage_order = ("ct", "go", "gi", "gf", "gc", "dcn", "cp")
+        stage_order = ("ct", "gi", "go", "gf", "gc", "dcn", "cp")
+        last_order = ("ct", "gi", "gc", "gf", "cp", "go", "dcn")
 
         offsets = keep.tile([P, WIDTH // 16], U16, name="offsets")
         ident = keep.tile([P, P], F32, name="ident")
@@ -53,7 +56,7 @@ def tile_attend_glstm_u_kernel(tc, wo, dy, dcn, gi, gf, go, gc, ct, cp, h0, offs
         places = {}
 
         def load_rows(name, j):
-            place = len(windows) * WINDOW_BYTES + (WINDOW_BYTES if (name, j) == ("gf", 2) else 0) + (2 * WINDOW_BYTES if ("gf", 2) in windows else 0)
+            place = len(windows) % WINDOWS * WINDOW_BYTES
             window = placed.tile([P, SESSIONS], F32, name="%s_%d" % (name, j), offset=place, align_bytes=64)
             nc.sync.dma_start(out=window[:], in_=tables[name][strip(j), :])
             windows[name, j] = window
@@ -70,11 +73,8 @@ def tile_attend_glstm_u_kernel(tc, wo, dy, dcn, gi, gf, go, gc, ct, cp, h0, offs
         def listed(name, j):
             return windows[name, j][:].indirect(offsets[:])
 
-        def quantized(name, columns, behind=None):
-            if behind is None:
-                codes = keep.tile([P, columns], U32, name=name + "_codes", align_bytes=64)
-            else:
-                codes = held([P, columns], U32, name + "_codes", behind, 0)
+        def quantized(name, columns):
+            codes = keep.tile([P, columns], U32, name=name + "_codes", align_bytes=64)
             scales = keep.tile([P, columns], U8, name=name + "_scales", align_bytes=64)
             return codes, scales
 
@@ -93,19 +93,22 @@ def tile_attend_glstm_u_kernel(tc, wo, dy, dcn, gi, gf, go, gc, ct, cp, h0, offs
                 stop=True,
             )
 
-        def bank(tag):
-            return psum.tile([P, WIDTH], F32, name="acc", tag=tag)
+        def bank():
+            return psum.tile([P, WIDTH], F32, name="acc", bufs=ACC_BANKS)
 
-        def quantize_along_m(raw, operand, fmt):
-            grouped = work.tile([P, WIDTH * PACK], BF16, name="grouped_m", align_bytes=64)
-            nc.vector.tensor_copy(
+        def quantize_along_m(raw, operand, cols, copy, fmt):
+            grouped = work.tile([P, (cols.stop - cols.start) * PACK], BF16, name="grouped_m", bufs=3, align_bytes=64)
+            copy(
                 out=grouped[:].rearrange("p (c i t) -> p c t i", i=NEIGHBOURS, t=PACK),
-                in_=raw[:].rearrange("p t (c i) -> p c t i", i=NEIGHBOURS),
+                in_=raw[:, :, cols].rearrange("p t (c i) -> p c t i", i=NEIGHBOURS),
             )
-            quantize(operand, whole, grouped[:], fmt)
+            quantize(operand, cols, grouped[:], fmt)
 
-        def turn(rows_bf16, count, copy, grouped, is_sorted=False):
-            turned = psum.tile([P, GATES, 2, P], F32, name="turned", bufs=TURN_BANKS)
+        def turn(rows_bf16, count, copy, grouped, is_sorted=False, own_bank=False):
+            if own_bank:
+                turned = psum.tile([P, GATES, 2, P], F32, name="turned_h0")
+            else:
+                turned = psum.tile([P, GATES, 2, P], F32, name="turned", bufs=TURN_BANKS)
             order = "p (g u w) -> p g u w" if is_sorted else "p (g w u) -> p g u w"
             words = rows_bf16[:].bitcast(F32).rearrange(order, g=count, u=2)
             for g in range(count):
@@ -123,7 +126,7 @@ def tile_attend_glstm_u_kernel(tc, wo, dy, dcn, gi, gf, go, gc, ct, cp, h0, offs
             nc.vector.tensor_tensor(out=out, in0=listed(name, j), in1=other, op=op)
 
         def row(name):
-            return work.tile([P, WIDTH], F32, name=name)
+            return work.tile([P, WIDTH], F32, name=name, bufs=TILES)
 
         def minus_one_times(out, in0, in1):
             nc.vector.scalar_tensor_tensor(out=out, in0=in0, scalar=1.0, in1=in1, op0=SUBTRACT, op1=MULT)
@@ -131,64 +134,38 @@ def tile_attend_glstm_u_kernel(tc, wo, dy, dcn, gi, gf, go, gc, ct, cp, h0, offs
         def negated_product(out, in0, in1):
             nc.vector.scalar_tensor_tensor(out=out, in0=in0, scalar=-1.0, in1=in1, op0=MULT, op1=MULT)
 
-        def quantize_old_hidden(k):
+        def old_hidden(k):
             rows = work.tile([P, WIDTH], BF16, name="old_hidden", bufs=TILES, align_bytes=64)
             picked("h0", k, rows[:])
-            grouped = work.tile([P, WIDTH], BF16, name="grouped_row", bufs=TILES, align_bytes=64)
-            turn(rows, 1, nc.vector.tensor_copy, grouped)
+            return rows
+
+        def quantize_old_hidden(k):
+            if 0 < k < last:
+                grouped = held([P, WIDTH], BF16, "grouped_h%d" % k, ("h0", k + 1), 0)
+            else:
+                grouped = work.tile([P, WIDTH], BF16, name="grouped_row", bufs=TILES, align_bytes=64)
+            turn(rows[k], 1, nc.vector.tensor_copy if k == 0 else nc.scalar.copy, grouped, own_bank=k < last)
             quantize(h0_q, strip(k), grouped[:], E4M3X4)
 
         def through_tanh(j):
             tanh_c = row("tanh_c")
             picked("ct", j, tanh_c[:])
             nc.scalar.activation(out=tanh_c[:], in_=tanh_c[:], func=SQUARE)
-            minus_back = row("minus_back")
-            minus_one_times(minus_back[:], tanh_c[:], dh[j][:])
-            return minus_back
+            minus_one_times(tanh_c[:], tanh_c[:], dh[j][:])
+            return tanh_c
 
-        def output_strip(j, g, tag):
-            acc = bank(tag)
-            for k in range(TILES):
-                product(acc[:, strip(k)], h0_q, strip(k), z_q[j], strip(g))
-            return acc[:].rearrange("p (k c) -> p k c", k=TILES)
-
-        def quantize_gradients(j, grouped, behind=None):
-            z_q.append(quantized("z%d" % j, GATES * P, behind))
-            quantize(z_q[j], slice(0, GATES * P), grouped[:], E5M2X4)
-
-        def store(g, cols, staged):
-            nc.sync.dma_start(out=outs[g][:, cols].rearrange("(k p) c -> p k c", p=P), in_=staged[:])
-
-        load_rows("h0", 0)
-        nc.sync.dma_start(out=offsets[:], in_=offs)
-        dy_raw = load_along_m(dy, "dy_raw")
-        wo_raw = load_along_m(wo, "wo_raw")
-        for k in range(1, TILES):
-            load_rows("h0", k)
-        for j in range(TILES):
-            for name in stage_order:
-                load_rows(name, j)
-
-        wo_q = quantized("wo", WIDTH)
-        dy_q = quantized("dy", WIDTH)
-        h0_q = quantized("h0", WIDTH)
-        z_q = []
-
-        quantize_old_hidden(0)
-        quantize_along_m(dy_raw, dy_q, E5M2X4)
-        quantize_along_m(wo_raw, wo_q, E4M3X4)
-        dh = [bank("dh%d" % j) for j in range(TILES)]
-        for j in range(TILES):
-            product(dh[j][:], wo_q, strip(j), dy_q, whole)
-        for k in range(1, TILES):
-            quantize_old_hidden(k)
+        def whole_rows(g, k, copy):
+            acc = bank()
+            product(acc[:], h0_q, strip(k), z_q[g], whole)
+            staged = work.tile([P, WIDTH], F32, name="staged", bufs=GATES * TILES)
+            copy(out=staged[:], in_=acc[:])
+            nc.sync.dma_start(out=outs[g][strip(k), :], in_=staged[:])
 
         def slope(name, j):
-            gate = row("gate")
+            gate = row("gate_" + name)
             picked(name, j, gate[:])
-            minus_slope = row("minus_slope_" + name)
-            minus_one_times(minus_slope[:], gate[:], gate[:])
-            return minus_slope
+            minus_one_times(gate[:], gate[:], gate[:])
+            return gate
 
         def sorted_words(rows):
             return rows.rearrange("p (u w e) -> p u w e", u=2, e=2)
@@ -196,61 +173,93 @@ def tile_attend_glstm_u_kernel(tc, wo, dy, dcn, gi, gf, go, gc, ct, cp, h0, offs
         def words_by_parity(rows):
             return rows.rearrange("p (w u e) -> p u w e", u=2, e=2)
 
-        pairs = []
-        turned_z = []
-        z = None
+        def quantize_gradients(j, z, behind):
+            grouped = held([P, GATES * WIDTH], BF16, "grouped_z%d" % j, behind, 0)
+            turn(z, GATES, nc.scalar.copy, grouped)
+            return grouped
+
+        load_rows("ct", 0)
+        nc.sync.dma_start(out=offsets[:], in_=offs)
+        dy_raw = load_along_m(dy, "dy_raw")
+        wo_raw = load_along_m(wo, "wo_raw")
+        for j in range(last):
+            for name in stage_order:
+                if (name, j) not in windows:
+                    load_rows(name, j)
+        for name in last_order:
+            load_rows(name, last)
+        for k in range(TILES):
+            load_rows("h0", k)
+
+        wo_q = quantized("wo", WIDTH)
+        dy_q = quantized("dy", WIDTH)
+        h0_q = quantized("h0", WIDTH)
+        z_q = [quantized("zi", WIDTH), quantized("zf", WIDTH)]
+
+        quantize_along_m(dy_raw, dy_q, whole, nc.vector.tensor_copy, E5M2X4)
+        quantize_along_m(wo_raw, wo_q, slice(0, WIDTH // 2), nc.vector.tensor_copy, E4M3X4)
+        quantize_along_m(wo_raw, wo_q, slice(WIDTH // 2, WIDTH), nc.scalar.copy, E4M3X4)
+        dh = [bank() for j in range(TILES)]
         for j in range(TILES):
+            product(dh[j][:], wo_q, strip(j), dy_q, whole)
+
+        z = None
+        for j in range(last):
             minus_back = through_tanh(j)
+            slope_i = slope("gi", j)
             gated = row("gated")
             picked_with("go", j, minus_back[:], MULT, gated[:])
-            slope_i = slope("gi", j)
-            if j >= 2:
-                quantize_gradients(j - 2, turned_z[j - 2], ("gi", j))
             slope_f = slope("gf", j)
-            if j >= 1:
-                turned_z.append(held([P, GATES * WIDTH], BF16, "grouped_z%d" % (j - 1), ("gf", j), HELD_BYTES // 2))
-                turn(z, GATES, nc.scalar.copy, turned_z[j - 1])
-            for g in range(GATES if j >= 2 else 0):
-                if j == 2:
-                    shift = HELD_BYTES // 2 - WINDOW_BYTES if g == 0 else HELD_BYTES + HELD_BYTES // 2
-                    pairs.append(held([P, TILES, 2 * P], F32, "staged_pair%d" % g, ("gf", j), shift))
-                nc.scalar.copy(out=pairs[g][:, :, strip(j - 2)], in_=output_strip(j - 2, g, "out%d" % g))
-                if j == last:
-                    store(g, slice(0, 2 * P), pairs[g])
-            minus_factor = row("minus_factor")
-            picked_with("gc", j, slope_i[:], MULT, minus_factor[:])
+            factors = work.tile([P, GATES, WIDTH], F32, name="factors", bufs=last)
+            picked_with("gc", j, slope_i[:], MULT, factors[:, 0, :])
             dc = row("dc")
-            picked_with("dcn", j, gated[:], SUBTRACT, dc[:])
-            if j == last:
-                quantize_gradients(j - 1, turned_z[j - 1])
-                accs = [output_strip(j - 1, g, "dh%d" % (g + GATES)) for g in range(GATES)]
-            negated_product(slope_f[:], slope_f[:], dc[:])
-            old_cell = row("old_cell")
-            if j < last:
-                z = work.tile([P, GATES * WIDTH], BF16, name="z", align_bytes=64)
-                negated_product(z[:, :WIDTH], minus_factor[:], dc[:])
-                picked("cp", j, old_cell[:])
-                nc.vector.tensor_tensor(out=z[:, WIDTH:], in0=old_cell[:], in1=slope_f[:], op=MULT)
+            picked("dcn", j, dc[:])
+            nc.vector.tensor_tensor(out=dc[:], in0=dc[:], in1=gated[:], op=SUBTRACT)
+            picked_with("cp", j, slope_f[:], MULT, factors[:, 1, :])
+            if j >= 1:
+                grouped = quantize_gradients(j - 1, z, ("dcn", j))
+                for g in range(GATES):
+                    quantize(z_q[g], strip(j - 1), grouped[:, g * WIDTH : (g + 1) * WIDTH], E5M2X4)
+            z = work.tile([P, GATES * WIDTH], BF16, name="z", bufs=last, align_bytes=64)
+            negated_product(
+                z[:].rearrange("p (g i) -> p g i", g=GATES),
+                factors[:],
+                dc[:].unsqueeze(1).to_broadcast([P, GATES, WIDTH]),
+            )
 
-        rows = [work.tile([P, WIDTH], BF16, name="z_last", align_bytes=64) for g in range(GATES)]
-        negated_product(rows[0][:], minus_factor[:], dc[:])
-        picked("cp", last, old_cell[:])
-        nc.vector.tensor_tensor(
-            out=sorted_words(rows[1][:]), in0=words_by_parity(old_cell[:]), in1=words_by_parity(slope_f[:]), op=MULT
-        )
-        z_q.append(quantized("z%d" % last, GATES * P))
+        minus_back = through_tanh(last)
+        gates = work.tile([P, GATES, WIDTH], F32, name="gates", bufs=1)
+        factors = work.tile([P, GATES, WIDTH], F32, name="last_factors", bufs=1)
+        for g, gate_name, partner in ((0, "gi", "gc"), (1, "gf", "cp")):
+            picked(gate_name, last, gates[:, g, :])
+            picked_with(partner, last, gates[:, g, :], MULT, factors[:, g, :])
+        grouped = quantize_gradients(last - 1, z, ("gf", last))
         for g in range(GATES):
-            staged = held([P, TILES, P], F32, "staged_strip%d" % g, ("cp", last), g * (HELD_BYTES + HELD_BYTES // 2))
-            nc.scalar.copy(out=staged[:], in_=accs[g])
-            store(g, strip(last - 1), staged)
-            if g == 0:
-                grouped = held([P, WIDTH], BF16, "grouped_zi", ("cp", last), HELD_BYTES)
-                turn(rows[g], 1, nc.scalar.copy, grouped)
-                quantize(z_q[last], strip(g), grouped[:], E5M2X4)
-        grouped = work.tile([P, WIDTH], BF16, name="grouped_row", bufs=TILES, align_bytes=64)
-        turn(rows[1], 1, nc.vector.tensor_copy, grouped, True)
-        quantize(z_q[last], strip(1), grouped[:], E5M2X4)
-        for g, copy in ((0, nc.scalar.copy), (1, nc.vector.tensor_copy)):
-            staged = work.tile([P, TILES, P], F32, name="staged_last")
-            copy(out=staged[:], in_=output_strip(last, g, "dh%d" % g))
-            store(g, strip(last), staged)
+            quantize(z_q[g], strip(last - 1), grouped[:, g * WIDTH : (g + 1) * WIDTH], E5M2X4)
+        minus_one_times(factors[:], gates[:], factors[:])
+        out_gate = row("gated")
+        picked("go", last, out_gate[:])
+        nc.vector.tensor_tensor(out=minus_back[:], in0=out_gate[:], in1=minus_back[:], op=MULT)
+        incoming = row("dc")
+        picked("dcn", last, incoming[:])
+        nc.vector.tensor_tensor(out=minus_back[:], in0=minus_back[:], in1=incoming[:], op=SUBTRACT)
+        z = []
+        for g in range(GATES):
+            z.append(work.tile([P, WIDTH], BF16, name="z_last", align_bytes=64))
+            nc.vector.tensor_tensor(
+                out=sorted_words(z[g][:]),
+                in0=words_by_parity(factors[:, g, :]),
+                in1=words_by_parity(minus_back[:]),
+                op=MULT,
+            )
+        rows = [old_hidden(k) for k in range(TILES)]
+        quantize_old_hidden(0)
+        for g in range(GATES):
+            grouped = work.tile([P, WIDTH], BF16, name="grouped_row", bufs=TILES, align_bytes=64)
+            turn(z[g], 1, nc.vector.tensor_copy, grouped, True)
+            quantize(z_q[g], strip(last), grouped[:], E5M2X4)
+        for k in range(TILES):
+            if k < last:
+                quantize_old_hidden(k + 1)
+            whole_rows(0, k, nc.scalar.copy if k == 2 else nc.vector.tensor_copy)
+            whole_rows(1, k, nc.scalar.copy if k >= 2 else nc.vector.tensor_copy)

@@ -155,8 +155,9 @@ def tile_attend_glstm_u_kernel(tc, wo, dy, dcn, gi, gf, go, gc, ct, cp, h0, offs
             return tanh_c
 
         def whole_rows(g, k, copy):
-            acc = bank()
-            product(acc[:], h0_q, strip(k), z_q[g], whole)
+            acc = psum.tile([P, WIDTH], F32, name="acc", tag="turned_h0") if (g, k) == (1, 1) else bank()
+            for cols in (slice(0, 2 * P), strip(2), strip(last)) if k == 0 else (whole,):
+                product(acc[:, cols], h0_q, strip(k), z_q[g], cols)
             staged = work.tile([P, WIDTH], F32, name="staged", bufs=GATES * TILES)
             copy(out=staged[:], in_=acc[:])
             nc.sync.dma_start(out=outs[g][strip(k), :], in_=staged[:])
@@ -261,5 +262,5 @@ def tile_attend_glstm_u_kernel(tc, wo, dy, dcn, gi, gf, go, gc, ct, cp, h0, offs
         for k in range(TILES):
             if k < last:
                 quantize_old_hidden(k + 1)
-            whole_rows(0, k, nc.scalar.copy if k == 2 else nc.vector.tensor_copy)
-            whole_rows(1, k, nc.scalar.copy if k >= 2 else nc.vector.tensor_copy)
+            whole_rows(0, k, nc.vector.tensor_copy)
+            whole_rows(1, k, nc.scalar.copy if k >= 1 else nc.vector.tensor_copy)

@@ -144,7 +144,7 @@ def tile_attend_glstm_u_kernel(tc, wo, dy, dcn, gi, gf, go, gc, ct, cp, h0, offs
                 grouped = held([P, WIDTH], BF16, "grouped_h%d" % k, ("h0", k + 1), 0)
             else:
                 grouped = work.tile([P, WIDTH], BF16, name="grouped_row", bufs=TILES, align_bytes=64)
-            turn(rows[k], 1, nc.vector.tensor_copy if k == 0 else nc.scalar.copy, grouped, own_bank=k < last)
+            turn(rows[k], 1, nc.scalar.copy if 0 < k < last else nc.vector.tensor_copy, grouped, own_bank=True)
             quantize(h0_q, strip(k), grouped[:], E4M3X4)
 
         def through_tanh(j):
@@ -155,10 +155,13 @@ def tile_attend_glstm_u_kernel(tc, wo, dy, dcn, gi, gf, go, gc, ct, cp, h0, offs
             return tanh_c
 
         def whole_rows(g, k, copy):
-            acc = psum.tile([P, WIDTH], F32, name="acc", tag="turned_h0") if (g, k) == (1, 1) else bank()
+            acc = bank()
             for cols in (slice(0, 2 * P), strip(2), strip(last)) if k == 0 else (whole,):
                 product(acc[:, cols], h0_q, strip(k), z_q[g], cols)
-            staged = work.tile([P, WIDTH], F32, name="staged", bufs=GATES * TILES)
+            if k == 1:
+                staged = held([P, WIDTH], F32, "staged_held%d" % g, ("h0", last), HELD_BYTES // 2 + g * HELD_BYTES)
+            else:
+                staged = work.tile([P, WIDTH], F32, name="staged", bufs=GATES * TILES)
             copy(out=staged[:], in_=acc[:])
             nc.sync.dma_start(out=outs[g][strip(k), :], in_=staged[:])
 
@@ -262,5 +265,5 @@ def tile_attend_glstm_u_kernel(tc, wo, dy, dcn, gi, gf, go, gc, ct, cp, h0, offs
         for k in range(TILES):
             if k < last:
                 quantize_old_hidden(k + 1)
-            whole_rows(0, k, nc.vector.tensor_copy)
-            whole_rows(1, k, nc.scalar.copy if k >= 1 else nc.vector.tensor_copy)
+            whole_rows(0, k, nc.scalar.copy if k >= 1 else nc.vector.tensor_copy)
+            whole_rows(1, k, nc.scalar.copy if k == 1 else nc.vector.tensor_copy)

@@ -26,7 +26,7 @@ TURN_BANKS = 2
 ACC_BANKS = 5
 WINDOWS = 21
 WINDOW_BYTES = 4 * SESSIONS
-HELD_BYTES = 4 * WIDTH
+ROW_BYTES = 4 * WIDTH
 FLOPS = 3 * 2 * WIDTH * WIDTH * WIDTH
 
 
@@ -42,7 +42,6 @@ def tile_attend_glstm_u_kernel(tc, wo, dy, dcn, gi, gf, go, gc, ct, cp, h0, offs
         outs = (out_0, out_1)
         tables = {"h0": h0, "ct": ct, "gi": gi, "gc": gc, "gf": gf, "cp": cp, "go": go, "dcn": dcn}
         stage_order = ("ct", "gi", "go", "gf", "gc", "dcn", "cp")
-        last_order = ("ct", "gi", "gc", "gf", "cp", "go", "dcn")
 
         offsets = keep.tile([P, WIDTH // 16], U16, name="offsets")
         ident = keep.tile([P, P], F32, name="ident")
@@ -131,21 +130,18 @@ def tile_attend_glstm_u_kernel(tc, wo, dy, dcn, gi, gf, go, gc, ct, cp, h0, offs
         def minus_one_times(out, in0, in1):
             nc.vector.scalar_tensor_tensor(out=out, in0=in0, scalar=1.0, in1=in1, op0=SUBTRACT, op1=MULT)
 
-        def negated_product(out, in0, in1):
-            nc.vector.scalar_tensor_tensor(out=out, in0=in0, scalar=-1.0, in1=in1, op0=MULT, op1=MULT)
-
         def old_hidden(k):
-            rows = work.tile([P, WIDTH], BF16, name="old_hidden", bufs=TILES, align_bytes=64)
-            picked("h0", k, rows[:])
-            return rows
+            gathered = work.tile([P, WIDTH], BF16, name="old_hidden", bufs=TILES, align_bytes=64)
+            picked("h0", k, gathered[:])
+            return gathered
 
-        def quantize_old_hidden(k):
+        def turn_old_hidden(k):
             if 0 < k < last:
                 grouped = held([P, WIDTH], BF16, "grouped_h%d" % k, ("h0", k + 1), 0)
             else:
                 grouped = work.tile([P, WIDTH], BF16, name="grouped_row", bufs=TILES, align_bytes=64)
-            turn(rows[k], 1, nc.scalar.copy if 0 < k < last else nc.vector.tensor_copy, grouped, own_bank=True)
-            quantize(h0_q, strip(k), grouped[:], E4M3X4)
+            turn(hidden[k], 1, nc.scalar.copy if 0 < k < last else nc.vector.tensor_copy, grouped, own_bank=True)
+            return grouped
 
         def through_tanh(j):
             tanh_c = row("tanh_c")
@@ -159,7 +155,7 @@ def tile_attend_glstm_u_kernel(tc, wo, dy, dcn, gi, gf, go, gc, ct, cp, h0, offs
             for cols in (slice(0, 2 * P), strip(2), strip(last)) if k == 0 else (whole,):
                 product(acc[:, cols], h0_q, strip(k), z_q[g], cols)
             if k == 1:
-                staged = held([P, WIDTH], F32, "staged_held%d" % g, ("h0", last), HELD_BYTES // 2 + g * HELD_BYTES)
+                staged = held([P, WIDTH], F32, "staged_held%d" % g, ("h0", last), ROW_BYTES // 2 + g * ROW_BYTES)
             else:
                 staged = work.tile([P, WIDTH], F32, name="staged", bufs=GATES * TILES)
             copy(out=staged[:], in_=acc[:])
@@ -171,27 +167,26 @@ def tile_attend_glstm_u_kernel(tc, wo, dy, dcn, gi, gf, go, gc, ct, cp, h0, offs
             minus_one_times(gate[:], gate[:], gate[:])
             return gate
 
-        def sorted_words(rows):
-            return rows.rearrange("p (u w e) -> p u w e", u=2, e=2)
+        def sorted_words(values):
+            return values.rearrange("p (u w e) -> p u w e", u=2, e=2)
 
-        def words_by_parity(rows):
-            return rows.rearrange("p (w u e) -> p u w e", u=2, e=2)
+        def words_by_parity(values):
+            return values.rearrange("p (w u e) -> p u w e", u=2, e=2)
 
         def quantize_gradients(j, z, behind):
             grouped = held([P, GATES * WIDTH], BF16, "grouped_z%d" % j, behind, 0)
             turn(z, GATES, nc.scalar.copy, grouped)
-            return grouped
+            for g in range(GATES):
+                quantize(z_q[g], strip(j), grouped[:, g * WIDTH : (g + 1) * WIDTH], E5M2X4)
 
         load_rows("ct", 0)
         nc.sync.dma_start(out=offsets[:], in_=offs)
         dy_raw = load_along_m(dy, "dy_raw")
         wo_raw = load_along_m(wo, "wo_raw")
-        for j in range(last):
+        for j in range(TILES):
             for name in stage_order:
                 if (name, j) not in windows:
                     load_rows(name, j)
-        for name in last_order:
-            load_rows(name, last)
         for k in range(TILES):
             load_rows("h0", k)
 
@@ -208,62 +203,54 @@ def tile_attend_glstm_u_kernel(tc, wo, dy, dcn, gi, gf, go, gc, ct, cp, h0, offs
             product(dh[j][:], wo_q, strip(j), dy_q, whole)
 
         z = None
-        for j in range(last):
+        for j in range(TILES):
             minus_back = through_tanh(j)
             slope_i = slope("gi", j)
             gated = row("gated")
             picked_with("go", j, minus_back[:], MULT, gated[:])
             slope_f = slope("gf", j)
-            factors = work.tile([P, GATES, WIDTH], F32, name="factors", bufs=last)
+            factors = work.tile([P, GATES, WIDTH], F32, name="factors", bufs=TILES)
             picked_with("gc", j, slope_i[:], MULT, factors[:, 0, :])
-            dc = row("dc")
-            picked("dcn", j, dc[:])
-            nc.vector.tensor_tensor(out=dc[:], in0=dc[:], in1=gated[:], op=SUBTRACT)
+            minus_dc = row("minus_dc")
+            picked("dcn", j, minus_dc[:])
+            nc.vector.tensor_tensor(out=minus_dc[:], in0=gated[:], in1=minus_dc[:], op=SUBTRACT)
             picked_with("cp", j, slope_f[:], MULT, factors[:, 1, :])
             if j >= 1:
-                grouped = quantize_gradients(j - 1, z, ("dcn", j))
-                for g in range(GATES):
-                    quantize(z_q[g], strip(j - 1), grouped[:, g * WIDTH : (g + 1) * WIDTH], E5M2X4)
-            z = work.tile([P, GATES * WIDTH], BF16, name="z", bufs=last, align_bytes=64)
-            negated_product(
-                z[:].rearrange("p (g i) -> p g i", g=GATES),
-                factors[:],
-                dc[:].unsqueeze(1).to_broadcast([P, GATES, WIDTH]),
-            )
+                quantize_gradients(j - 1, z, ("dcn", j))
+            if j < last:
+                z = work.tile([P, GATES * WIDTH], BF16, name="z", bufs=last, align_bytes=64)
+                nc.vector.tensor_tensor(
+                    out=z[:].rearrange("p (g i) -> p g i", g=GATES),
+                    in0=factors[:],
+                    in1=minus_dc[:].unsqueeze(1).to_broadcast([P, GATES, WIDTH]),
+                    op=MULT,
+                )
 
-        minus_back = through_tanh(last)
-        gates = work.tile([P, GATES, WIDTH], F32, name="gates", bufs=1)
-        factors = work.tile([P, GATES, WIDTH], F32, name="last_factors", bufs=1)
-        for g, gate_name, partner in ((0, "gi", "gc"), (1, "gf", "cp")):
-            picked(gate_name, last, gates[:, g, :])
-            picked_with(partner, last, gates[:, g, :], MULT, factors[:, g, :])
-        grouped = quantize_gradients(last - 1, z, ("gf", last))
-        for g in range(GATES):
-            quantize(z_q[g], strip(last - 1), grouped[:, g * WIDTH : (g + 1) * WIDTH], E5M2X4)
-        minus_one_times(factors[:], gates[:], factors[:])
-        out_gate = row("gated")
-        picked("go", last, out_gate[:])
-        nc.vector.tensor_tensor(out=minus_back[:], in0=out_gate[:], in1=minus_back[:], op=MULT)
-        incoming = row("dc")
-        picked("dcn", last, incoming[:])
-        nc.vector.tensor_tensor(out=minus_back[:], in0=minus_back[:], in1=incoming[:], op=SUBTRACT)
-        z = []
-        for g in range(GATES):
-            z.append(work.tile([P, WIDTH], BF16, name="z_last", align_bytes=64))
+        def last_gradient(g, out):
             nc.vector.tensor_tensor(
-                out=sorted_words(z[g][:]),
+                out=sorted_words(out[:]),
                 in0=words_by_parity(factors[:, g, :]),
-                in1=words_by_parity(minus_back[:]),
+                in1=words_by_parity(minus_dc[:]),
                 op=MULT,
             )
-        rows = [old_hidden(k) for k in range(TILES)]
-        quantize_old_hidden(0)
-        for g in range(GATES):
+
+        def turn_last(z_row):
             grouped = work.tile([P, WIDTH], BF16, name="grouped_row", bufs=TILES, align_bytes=64)
-            turn(z[g], 1, nc.vector.tensor_copy, grouped, True)
-            quantize(z_q[g], strip(last), grouped[:], E5M2X4)
+            turn(z_row, 1, nc.vector.tensor_copy, grouped, is_sorted=True)
+            return grouped
+
+        hidden = [old_hidden(k) for k in range(TILES)]
+        zi = held([P, WIDTH], BF16, "zi_last", ("h0", 0), 0)
+        last_gradient(0, zi)
+        grouped_h0 = turn_old_hidden(0)
+        zf = held([P, WIDTH], BF16, "zf_last", ("h0", 0), ROW_BYTES // 2)
+        last_gradient(1, zf)
+        grouped_zi = turn_last(zi)
+        quantize(h0_q, strip(0), grouped_h0[:], E4M3X4)
+        quantize(z_q[0], strip(last), grouped_zi[:], E5M2X4)
+        quantize(z_q[1], strip(last), turn_last(zf)[:], E5M2X4)
         for k in range(TILES):
             if k < last:
-                quantize_old_hidden(k + 1)
+                quantize(h0_q, strip(k + 1), turn_old_hidden(k + 1)[:], E4M3X4)
             whole_rows(0, k, nc.scalar.copy if k >= 1 else nc.vector.tensor_copy)
             whole_rows(1, k, nc.scalar.copy if k == 1 else nc.vector.tensor_copy)

@@ -121,8 +121,8 @@ def tile_attend_glstm_u_kernel(tc, wo, dy, dcn, gi, gf, go, gc, ct, cp, h0, offs
         def picked(name, j, out):
             nc.scalar.activation(out=out, in_=listed(name, j), func=COPY)
 
-        def picked_with(name, j, other, op, out):
-            nc.vector.tensor_tensor(out=out, in0=listed(name, j), in1=other, op=op)
+        def picked_times(name, j, other, out):
+            nc.vector.tensor_tensor(out=out, in0=listed(name, j), in1=other, op=MULT)
 
         def row(name):
             return work.tile([P, WIDTH], F32, name=name, bufs=TILES)
@@ -136,11 +136,11 @@ def tile_attend_glstm_u_kernel(tc, wo, dy, dcn, gi, gf, go, gc, ct, cp, h0, offs
             return gathered
 
         def turn_old_hidden(k):
-            if 0 < k < last:
+            if k == 1:
                 grouped = held([P, WIDTH], BF16, "grouped_h%d" % k, ("h0", k + 1), 0)
             else:
                 grouped = work.tile([P, WIDTH], BF16, name="grouped_row", bufs=TILES, align_bytes=64)
-            turn(hidden[k], 1, nc.scalar.copy if 0 < k < last else nc.vector.tensor_copy, grouped, own_bank=True)
+            turn(hidden[k], 1, nc.scalar.copy if k == 1 else nc.vector.tensor_copy, grouped, own_bank=True)
             return grouped
 
         def through_tanh(j):
@@ -150,18 +150,21 @@ def tile_attend_glstm_u_kernel(tc, wo, dy, dcn, gi, gf, go, gc, ct, cp, h0, offs
             minus_one_times(tanh_c[:], tanh_c[:], dh[j][:])
             return tanh_c
 
+        behind_gathers = [(1, 0), (0, 1), (1, 1)]
+
         def whole_rows(g, k, copy):
             acc = bank()
             for cols in (slice(0, 2 * P), strip(2), strip(last)) if k == 0 else (whole,):
                 product(acc[:, cols], h0_q, strip(k), z_q[g], cols)
-            if k == 1:
-                staged = held([P, WIDTH], F32, "staged_held%d" % g, ("h0", last), ROW_BYTES // 2 + g * ROW_BYTES)
+            if (g, k) in behind_gathers:
+                shift = behind_gathers.index((g, k)) * ROW_BYTES - ROW_BYTES // 2
+                staged = held([P, WIDTH], F32, "staged_held%d%d" % (g, k), ("h0", last), shift)
             else:
                 staged = work.tile([P, WIDTH], F32, name="staged", bufs=GATES * TILES)
             copy(out=staged[:], in_=acc[:])
             nc.sync.dma_start(out=outs[g][strip(k), :], in_=staged[:])
 
-        def slope(name, j):
+        def minus_slope(name, j):
             gate = row("gate_" + name)
             picked(name, j, gate[:])
             minus_one_times(gate[:], gate[:], gate[:])
@@ -205,16 +208,16 @@ def tile_attend_glstm_u_kernel(tc, wo, dy, dcn, gi, gf, go, gc, ct, cp, h0, offs
         z = None
         for j in range(TILES):
             minus_back = through_tanh(j)
-            slope_i = slope("gi", j)
+            minus_slope_i = minus_slope("gi", j)
             gated = row("gated")
-            picked_with("go", j, minus_back[:], MULT, gated[:])
-            slope_f = slope("gf", j)
+            picked_times("go", j, minus_back[:], gated[:])
+            minus_slope_f = minus_slope("gf", j)
             factors = work.tile([P, GATES, WIDTH], F32, name="factors", bufs=TILES)
-            picked_with("gc", j, slope_i[:], MULT, factors[:, 0, :])
+            picked_times("gc", j, minus_slope_i[:], factors[:, 0, :])
             minus_dc = row("minus_dc")
             picked("dcn", j, minus_dc[:])
             nc.vector.tensor_tensor(out=minus_dc[:], in0=gated[:], in1=minus_dc[:], op=SUBTRACT)
-            picked_with("cp", j, slope_f[:], MULT, factors[:, 1, :])
+            picked_times("cp", j, minus_slope_f[:], factors[:, 1, :])
             if j >= 1:
                 quantize_gradients(j - 1, z, ("dcn", j))
             if j < last:
@@ -249,8 +252,12 @@ def tile_attend_glstm_u_kernel(tc, wo, dy, dcn, gi, gf, go, gc, ct, cp, h0, offs
         quantize(h0_q, strip(0), grouped_h0[:], E4M3X4)
         quantize(z_q[0], strip(last), grouped_zi[:], E5M2X4)
         quantize(z_q[1], strip(last), turn_last(zf)[:], E5M2X4)
-        for k in range(TILES):
-            if k < last:
-                quantize(h0_q, strip(k + 1), turn_old_hidden(k + 1)[:], E4M3X4)
-            whole_rows(0, k, nc.scalar.copy if k >= 1 else nc.vector.tensor_copy)
-            whole_rows(1, k, nc.scalar.copy if k == 1 else nc.vector.tensor_copy)
+        quantize(h0_q, strip(1), turn_old_hidden(1)[:], E4M3X4)
+        whole_rows(0, 0, nc.vector.tensor_copy)
+        for k in range(2, TILES):
+            quantize(h0_q, strip(k), turn_old_hidden(k)[:], E4M3X4)
+        for g, k in behind_gathers:
+            whole_rows(g, k, nc.scalar.copy)
+        for k in range(2, TILES):
+            whole_rows(0, k, nc.vector.tensor_copy)
+            whole_rows(1, k, nc.scalar.copy)

@@ -159,8 +159,10 @@ def tile_attend_glstm_u_kernel(tc, wo, dy, dcn, gi, gf, go, gc, ct, cp, h0, offs
             if (g, k) in behind_gathers:
                 shift = behind_gathers.index((g, k)) * ROW_BYTES - ROW_BYTES // 2
                 staged = held([P, WIDTH], F32, "staged_held%d%d" % (g, k), ("h0", last), shift)
+            elif k == 0:
+                staged = held([P, WIDTH], F32, "staged_first", ("ct", last), 0)
             else:
-                staged = work.tile([P, WIDTH], F32, name="staged", bufs=GATES * TILES)
+                staged = work.tile([P, WIDTH], F32, name="staged", bufs=TILES)
             copy(out=staged[:], in_=acc[:])
             nc.sync.dma_start(out=outs[g][strip(k), :], in_=staged[:])
 
@@ -237,8 +239,8 @@ def tile_attend_glstm_u_kernel(tc, wo, dy, dcn, gi, gf, go, gc, ct, cp, h0, offs
                 op=MULT,
             )
 
-        def turn_last(z_row):
-            grouped = work.tile([P, WIDTH], BF16, name="grouped_row", bufs=TILES, align_bytes=64)
+        def turn_last(g, z_row):
+            grouped = held([P, WIDTH], BF16, "grouped_last%d" % g, ("ct", last), (1 - g) * ROW_BYTES)
             turn(z_row, 1, nc.vector.tensor_copy, grouped, is_sorted=True)
             return grouped
 
@@ -248,16 +250,17 @@ def tile_attend_glstm_u_kernel(tc, wo, dy, dcn, gi, gf, go, gc, ct, cp, h0, offs
         grouped_h0 = turn_old_hidden(0)
         zf = held([P, WIDTH], BF16, "zf_last", ("h0", 0), ROW_BYTES // 2)
         last_gradient(1, zf)
-        grouped_zi = turn_last(zi)
+        grouped_zi = turn_last(0, zi)
         quantize(h0_q, strip(0), grouped_h0[:], E4M3X4)
         quantize(z_q[0], strip(last), grouped_zi[:], E5M2X4)
-        quantize(z_q[1], strip(last), turn_last(zf)[:], E5M2X4)
+        quantize(z_q[1], strip(last), turn_last(1, zf)[:], E5M2X4)
         quantize(h0_q, strip(1), turn_old_hidden(1)[:], E4M3X4)
         whole_rows(0, 0, nc.vector.tensor_copy)
+        whole_rows(1, 0, nc.scalar.copy)
         for k in range(2, TILES):
             quantize(h0_q, strip(k), turn_old_hidden(k)[:], E4M3X4)
-        for g, k in behind_gathers:
-            whole_rows(g, k, nc.scalar.copy)
+        for g in range(GATES):
+            whole_rows(g, 1, nc.scalar.copy)
         for k in range(2, TILES):
             whole_rows(0, k, nc.vector.tensor_copy)
             whole_rows(1, k, nc.scalar.copy)

from contextlib import ExitStack

import concourse.mybir as mybir
from concourse.masks import make_identity

F32 = mybir.dt.float32
BF16 = mybir.dt.bfloat16
U32 = mybir.dt.uint32
U16 = mybir.dt.uint16
U8 = mybir.dt.uint8
E4M3X4 = mybir.dt.float8_e4m3fn_x4
E5M2X4 = mybir.dt.float8_e5m2_x4
MULT = mybir.AluOpType.mult
SUBTRACT = mybir.AluOpType.subtract
COPY = mybir.ActivationFunctionType.Copy
SQUARE = mybir.ActivationFunctionType.Square

P = 128
PACK = 4
WIDTH = 512
SESSIONS = 1024
TILES = WIDTH // P
GATES = 2
NEIGHBOURS = 4
TURN_BANKS = 2
ACC_BANKS = 5
WINDOWS = 21
WINDOW_BYTES = 4 * SESSIONS
ROW_BYTES = 4 * WIDTH
FLOPS = 3 * 2 * WIDTH * WIDTH * WIDTH


def tile_attend_glstm_u_kernel(tc, wo, dy, dcn, gi, gf, go, gc, ct, cp, h0, offs, out_0, out_1):
    nc = tc.nc
    with ExitStack() as ctx:
        keep = ctx.enter_context(tc.tile_pool(name="keep", bufs=1))
        placed = ctx.enter_context(tc.tile_pool(name="placed", bufs=1))
        work = ctx.enter_context(tc.tile_pool(name="work", bufs=2))
        psum = ctx.enter_context(tc.psum_pool(name="psum", bufs=1))

        last = TILES - 1
        outs = (out_0, out_1)
        tables = {"h0": h0, "ct": ct, "gi": gi, "gc": gc, "gf": gf, "cp": cp, "go": go, "dcn": dcn}
        stage_order = ("ct", "gi", "go", "gf", "gc", "dcn", "cp")

        offsets = keep.tile([P, WIDTH // 16], U16, name="offsets")
        ident = keep.tile([P, P], F32, name="ident")
        make_identity(nc, ident[:])

        def strip(j):
            return slice(j * P, (j + 1) * P)

        whole = slice(0, WIDTH)
        windows = {}
        places = {}

        def load_rows(name, j):
            place = len(windows) % WINDOWS * WINDOW_BYTES
            window = placed.tile([P, SESSIONS], F32, name="%s_%d" % (name, j), offset=place, align_bytes=64)
            nc.sync.dma_start(out=window[:], in_=tables[name][strip(j), :])
            windows[name, j] = window
            places[name, j] = place

        def load_along_m(src, name):
            raw = keep.tile([P, PACK, WIDTH], F32, name=name)
            nc.sync.dma_start(out=raw[:], in_=src.rearrange("(p t) c -> p t c", t=PACK))
            return raw

        def held(shape, dtype, name, behind, shift):
            return placed.tile(shape, dtype, name=name, offset=places[behind] + shift, align_bytes=64)

        def listed(name, j):
            return windows[name, j][:].indirect(offsets[:])

        def quantized(name, columns):
            codes = keep.tile([P, columns], U32, name=name + "_codes", align_bytes=64)
            scales = keep.tile([P, columns], U8, name=name + "_scales", align_bytes=64)
            return codes, scales

        def quantize(operand, cols, grouped, fmt):
            codes, scales = operand
            nc.vector.quantize_mx(out=codes[:, cols].bitcast(fmt), scales=scales[:, cols], in_=grouped)

        def product(acc, lhs, lhs_cols, rhs, rhs_cols):
            nc.tensor.matmul_mx(
                out=acc,
                lhsT=lhs[0][:, lhs_cols].bitcast(E4M3X4),
                lhsT_scale=lhs[1][:, lhs_cols],
                rhs=rhs[0][:, rhs_cols].bitcast(E5M2X4),
                rhs_scale=rhs[1][:, rhs_cols],
                start=True,
                stop=True,
            )

        def bank():
            return psum.tile([P, WIDTH], F32, name="acc", bufs=ACC_BANKS)

        def quantize_along_m(raw, operand, cols, copy, fmt):
            grouped = work.tile([P, (cols.stop - cols.start) * PACK], BF16, name="grouped_m", bufs=3, align_bytes=64)
            copy(
                out=grouped[:].rearrange("p (c i t) -> p c t i", i=NEIGHBOURS, t=PACK),
                in_=raw[:, :, cols].rearrange("p t (c i) -> p c t i", i=NEIGHBOURS),
            )
            quantize(operand, cols, grouped[:], fmt)

        def turn(rows_bf16, count, copy, grouped, is_sorted=False, own_bank=False):
            if own_bank:
                turned = psum.tile([P, GATES, 2, P], F32, name="turned_h0")
            else:
                turned = psum.tile([P, GATES, 2, P], F32, name="turned", bufs=TURN_BANKS)
            order = "p (g u w) -> p g u w" if is_sorted else "p (g w u) -> p g u w"
            words = rows_bf16[:].bitcast(F32).rearrange(order, g=count, u=2)
            for g in range(count):
                for u in range(2):
                    nc.tensor.transpose(turned[:, g, u, :], words[:, g, u, :], ident[:])
            copy(
                out=grouped[:].bitcast(F32).rearrange("p (g c u) -> p g c u", g=count, u=2),
                in_=turned[:, :count, :, :].rearrange("p g u c -> p g c u"),
            )

        def picked(name, j, out):
            nc.scalar.activation(out=out, in_=listed(name, j), func=COPY)

        def picked_times(name, j, other, out):
            nc.vector.tensor_tensor(out=out, in0=listed(name, j), in1=other, op=MULT)

        def row(name):
            return work.tile([P, WIDTH], F32, name=name, bufs=TILES)

        def minus_one_times(out, in0, in1):
            nc.vector.scalar_tensor_tensor(out=out, in0=in0, scalar=1.0, in1=in1, op0=SUBTRACT, op1=MULT)

        def old_hidden(k):
            gathered = work.tile([P, WIDTH], BF16, name="old_hidden", bufs=TILES, align_bytes=64)
            picked("h0", k, gathered[:])
            return gathered

        def turn_old_hidden(k):
            if k == 1:
                grouped = held([P, WIDTH], BF16, "grouped_h%d" % k, ("h0", k + 1), 0)
            else:
                grouped = work.tile([P, WIDTH], BF16, name="grouped_row", bufs=TILES, align_bytes=64)
            turn(hidden[k], 1, nc.scalar.copy if k == 1 else nc.vector.tensor_copy, grouped, own_bank=True)
            return grouped

        def through_tanh(j):
            tanh_c = row("tanh_c")
            picked("ct", j, tanh_c[:])
            nc.scalar.activation(out=tanh_c[:], in_=tanh_c[:], func=SQUARE)
            minus_one_times(tanh_c[:], tanh_c[:], dh[j][:])
            return tanh_c

        behind_gathers = [(1, 0), (0, 1), (1, 1)]

        def whole_rows(g, k, copy):
            acc = bank()
            for cols in (slice(0, 2 * P), strip(2), strip(last)) if k == 0 else (whole,):
                product(acc[:, cols], h0_q, strip(k), z_q[g], cols)
            if (g, k) in behind_gathers:
                shift = behind_gathers.index((g, k)) * ROW_BYTES - ROW_BYTES // 2
                staged = held([P, WIDTH], F32, "staged_held%d%d" % (g, k), ("h0", last), shift)
            elif k == 0:
                staged = held([P, WIDTH], F32, "staged_first", ("ct", last), 0)
            else:
                staged = work.tile([P, WIDTH], F32, name="staged", bufs=TILES)
            copy(out=staged[:], in_=acc[:])
            nc.sync.dma_start(out=outs[g][strip(k), :], in_=staged[:])

        def minus_slope(name, j):
            gate = row("gate_" + name)
            picked(name, j, gate[:])
            minus_one_times(gate[:], gate[:], gate[:])
            return gate

        def sorted_words(values):
            return values.rearrange("p (u w e) -> p u w e", u=2, e=2)

        def words_by_parity(values):
            return values.rearrange("p (w u e) -> p u w e", u=2, e=2)

        def quantize_gradients(j, z, behind):
            grouped = held([P, GATES * WIDTH], BF16, "grouped_z%d" % j, behind, 0)
            turn(z, GATES, nc.scalar.copy, grouped)
            for g in range(GATES):
                quantize(z_q[g], strip(j), grouped[:, g * WIDTH : (g + 1) * WIDTH], E5M2X4)

        load_rows("ct", 0)
        nc.sync.dma_start(out=offsets[:], in_=offs)
        dy_raw = load_along_m(dy, "dy_raw")
        wo_raw = load_along_m(wo, "wo_raw")
        for j in range(TILES):
            for name in stage_order:
                if (name, j) not in windows:
                    load_rows(name, j)
        for k in range(TILES):
            load_rows("h0", k)

        wo_q = quantized("wo", WIDTH)
        dy_q = quantized("dy", WIDTH)
        h0_q = quantized("h0", WIDTH)
        z_q = [quantized("zi", WIDTH), quantized("zf", WIDTH)]

        quantize_along_m(dy_raw, dy_q, whole, nc.vector.tensor_copy, E5M2X4)
        quantize_along_m(wo_raw, wo_q, slice(0, WIDTH // 2), nc.vector.tensor_copy, E4M3X4)
        quantize_along_m(wo_raw, wo_q, slice(WIDTH // 2, WIDTH), nc.scalar.copy, E4M3X4)
        dh = [bank() for j in range(TILES)]
        for j in range(TILES):
            product(dh[j][:], wo_q, strip(j), dy_q, whole)

        z = None
        for j in range(TILES):
            minus_back = through_tanh(j)
            minus_slope_i = minus_slope("gi", j)
            gated = row("gated")
            picked_times("go", j, minus_back[:], gated[:])
            minus_slope_f = minus_slope("gf", j)
            factors = work.tile([P, GATES, WIDTH], F32, name="factors", bufs=TILES)
            picked_times("gc", j, minus_slope_i[:], factors[:, 0, :])
            minus_dc = row("minus_dc")
            picked("dcn", j, minus_dc[:])
            nc.vector.tensor_tensor(out=minus_dc[:], in0=gated[:], in1=minus_dc[:], op=SUBTRACT)
            picked_times("cp", j, minus_slope_f[:], factors[:, 1, :])
            if j >= 1:
                quantize_gradients(j - 1, z, ("dcn", j))
            if j < last:
                z = work.tile([P, GATES * WIDTH], BF16, name="z", bufs=last, align_bytes=64)
                nc.vector.tensor_tensor(
                    out=z[:].rearrange("p (g i) -> p g i", g=GATES),
                    in0=factors[:],
                    in1=minus_dc[:].unsqueeze(1).to_broadcast([P, GATES, WIDTH]),
                    op=MULT,
                )

        def last_gradient(g, out):
            nc.vector.tensor_tensor(
                out=sorted_words(out[:]),
                in0=words_by_parity(factors[:, g, :]),
                in1=words_by_parity(minus_dc[:]),
                op=MULT,
            )

        def turn_last(g, z_row):
            grouped = held([P, WIDTH], BF16, "grouped_last%d" % g, ("ct", last), (1 - g) * ROW_BYTES)
            turn(z_row, 1, nc.vector.tensor_copy, grouped, is_sorted=True)
            return grouped

        hidden = [old_hidden(k) for k in range(TILES)]
        zi = held([P, WIDTH], BF16, "zi_last", ("h0", 0), 0)
        last_gradient(0, zi)
        grouped_h0 = turn_old_hidden(0)
        zf = held([P, WIDTH], BF16, "zf_last", ("h0", 0), ROW_BYTES // 2)
        last_gradient(1, zf)
        grouped_zi = turn_last(0, zi)
        quantize(h0_q, strip(0), grouped_h0[:], E4M3X4)
        quantize(z_q[0], strip(last), grouped_zi[:], E5M2X4)
        quantize(z_q[1], strip(last), turn_last(1, zf)[:], E5M2X4)
        quantize(h0_q, strip(1), turn_old_hidden(1)[:], E4M3X4)
        whole_rows(0, 0, nc.vector.tensor_copy)
        whole_rows(1, 0, nc.scalar.copy)
        for k in range(2, TILES):
            quantize(h0_q, strip(k), turn_old_hidden(k)[:], E4M3X4)
        for g in range(GATES):
            whole_rows(g, 1, nc.scalar.copy)
        for k in range(2, TILES):
            whole_rows(0, k, nc.vector.tensor_copy)
            whole_rows(1, k, nc.scalar.copy)
